import numpy as np, ml_dtypes
CORES = [242,247,114,119]
N = 4
BF = ml_dtypes.bfloat16
W, V, L, F, B, TH, S, RO, SV = 2048, 512, 256, 4, 2, 9, 2, 3, 2
def parts(rng):
    x = np.clip(rng.integers(0, 256, (N, 8, 1, W)) + rng.integers(-70, 71, (N, 8, 16, W)), 0, 255)
    q = np.clip(rng.integers(0, 200, (N, 8, 1, L)) + rng.integers(-70, 71, (N, 8, 16, L)), 0, 255)
    return x, q, rng.integers(0, W, (N, 8, W)), rng.integers(0, W, (N, 8, W)), rng.integers(0, V, (N, 8, W)), rng.integers(0, W, (N, 8, 16, V))
def pack(x, q, nx, pv, rc, u):
    return {"xd": np.ascontiguousarray(x.reshape(N, 128, W)).astype(np.float32).astype(BF), "nx": nx.astype(np.int32), "pv": pv.astype(np.int32), "rc": rc.astype(np.int32),
            "ul": np.ascontiguousarray(u.reshape(N, 128, V)).astype(np.int32), "mv": np.ascontiguousarray(q.reshape(N, 128, L)).astype(np.float32).astype(BF)}
def some(rng, n):
    return 255 * (np.argsort(rng.random((N, 8, 16, L)), axis=2) < n[:, :, None, :])
def setup_inputs(rng):
    return pack(*parts(rng))
def setup_inputs_corners(rng):
    x, q, nx, pv, rc, u = parts(rng); c = np.arange(W); sh = int(rng.integers(0, 8))
    x[..., ::64] = 255; x[..., 63::64] = 0; q[..., :8] = 0; q[..., L - 8:] = 255
    for r in range(N):
        for g in range(8):
            k = (g + 3 * r + sh) % 8
            if k == 0: nx[r, g] = c; pv[r, g] = c; rc[r, g] = c % V
            elif k == 1: nx[r, g] = np.minimum(c + 1, W - 1); pv[r, g] = np.maximum(c - 1, 0); rc[r, g] = V - 1 - c % V
            elif k == 2: nx[r, g] = (c + 1) % W; pv[r, g] = (c + W - 1) % W
            elif k == 3: nx[r, g] = 0; pv[r, g] = W - 1; rc[r, g] = V - 1
            elif k == 4: nx[r, g] = W - 1; pv[r, g] = 0; rc[r, g] = 0
            elif k == 5: u[r, g] = u[r, g, :1] + np.zeros((16, 1), np.int64)
            elif k == 6: u[r, g] = rng.choice(np.array([0, W - 1, W // 2]), (16, V))
            else: nx[r, g] = c ^ 1; pv[r, g] = c ^ 1
            if (g + r) % 2 == 0:
                z, p, e, t1, t2, t3 = [int(b) for b in 1 + rng.permutation(W - 2)[:6]]; xb, ub, i = x[r, g], u[r, g], int(rng.integers(0, 16))
                xb[:, [z, p]] = 0; xb[i, p] = 1; xb[:, [e, t1, t2, t3]] = 255; xb[i, e] = 254
                nx[r, g, [z, p, t1, t2, t3]] = z; pv[r, g, [z, t1, t3]] = t1; pv[r, g, [p, e, t2]] = t2
                ub[:, (L - 1) * SV] = p; ub[15, (L - 1) * SV] = z
                ub[:, (L - 2) * SV] = t3
                ub[:, SV] = t1; ub[15, SV] = e
    return pack(x, q, nx, pv, rc, u)
def setup_inputs_counts(rng):
    x, q, nx, pv, rc, u = parts(rng); x = np.clip(x, 1, 254)
    much = rng.permutation(np.array((256, 511, 1024, 8 * L - 1, 255, 257, 8 * L, 0)[:N]))
    hit = (np.argsort(rng.random((N, 8 * L)), axis=1) < much[:, None]).reshape(N, 8, L)
    n = np.where(hit, rng.integers(TH, 17, (N, 8, L)), rng.integers(0, TH, (N, 8, L)))
    return pack(x, some(rng, n), nx, pv, rc, u)
def setup_inputs_ends(rng):
    x = 255 * rng.integers(0, 2, (N, 8, 16, W)); m = rng.random((N, 8, 1, W)); x = np.where(m < 0.3, 0, np.where(m < 0.6, 255, x))
    fl = rng.integers(0, 2, (N, 8)); fl[0] = 0; fl[N - 1] = 0; f2 = rng.integers(0, 2, (N, 8))
    x[:, :, :, 0] = 255 * fl[:, :, None]; x[:, :, :, W - 1] = 255 * (1 - fl)[:, :, None]
    odd = (np.arange(8) % 2 == 1)[None, :, None]
    def far(hi, n):
        a = hi * rng.integers(0, 2, (N, 8, n))
        return np.where((rng.random((N, 8, n)) < 0.35) & odd, rng.integers(0, hi + 1, (N, 8, n)), a)
    nx = far(W - 1, W); pv = far(W - 1, W); rc = far(V - 1, W); u = far(W - 1, 16 * V).reshape(N, 8, 16, V)
    u[N - 1] = (W - 1) * rng.integers(0, 2, (8, 16, V)); nx[N - 1, :, 0] = 0; nx[N - 1, :, W - 1] = 0
    rc[:, :, 0] = (V - 1) * f2; rc[:, :, W - 1] = (V - 1) * (1 - f2)
    n = rng.choice(np.array([0, TH - 1, TH, 16]), (N, 8, L))
    n[0] = rng.choice(np.array([0, TH - 1, TH // 2]), (8, L)); n[N - 1] = rng.choice(np.array([16, TH]), (8, L))
    z = (L - 1) * SV; n[0, 7, L - 2:] = 0; n[N - 1, 7, L - 1] = 16
    u[0, 7, :, z] = W - 1; u[0, 7, :, z - SV] = W - 1; u[0, 7, 15, z - SV] = 0
    u[N - 1, 7, :, z] = W - 1; u[N - 1, 7, 15, z] = 0
    n[1, 7, L - 1] = 16; x[1, 7, :, 0] = 0; x[1, 7, :, 1] = 255; x[1, 7, :, 2] = 0; x[1, 7, :, W - 1] = 255
    nx[1, 7, 0] = W - 1; nx[1, 7, W - 1] = W - 1; nx[1, 7, 1] = 2; u[1, 7, :15, z] = 1; u[1, 7, 15, z] = 0
    return pack(x, some(rng, n), nx, pv, rc, u)
def setup_inputs_near(rng):
    x, q, nx, pv, rc, u = parts(rng); b = rng.integers(0, 255, (N, 8, 1, 1)); b[0, 0] = 0; b[1, 1] = 254
    x = b + (rng.random((N, 8, 16, W)) < rng.choice(np.array([0.2, 0.5, 0.8]), (N, 8, 1, W)))
    q = b + (rng.random((N, 8, 16, L)) < rng.choice(np.array([0.2, 0.5, 0.8, 1.0]), (N, 8, 1, L)))
    few = rng.integers(0, W, (N, 8, 64)); u = np.take_along_axis(few, rng.integers(0, 64, (N, 8, 16 * V)), 2).reshape(N, 8, 16, V)
    return pack(x, q, nx, pv, rc, u)
def setup_inputs_spread(rng):
    x = (np.exp2(8 * rng.random((N, 8, 1, W))) * rng.random((N, 8, 16, W))).astype(np.int64)
    q = (np.exp2(8 * rng.random((N, 8, 1, L))) * rng.random((N, 8, 16, L))).astype(np.int64)
    def skew(hi, n):
        return np.minimum((hi * rng.random((N, 8, n)) ** rng.choice(np.array([1, 2, 4]), (N, 8, 1))).astype(np.int64), hi - 1)
    return pack(np.minimum(x, 255), np.minimum(q, 255), skew(W, W), skew(W, W), skew(V, W), skew(W, 16 * V).reshape(N, 8, 16, V))
def check_inputs(d):
    bad = []
    for k, lo, hi in (("xd", 0, 255), ("nx", 0, W - 1), ("pv", 0, W - 1), ("rc", 0, V - 1), ("ul", 0, W - 1), ("mv", 0, 255)):
        a = np.asarray(d[k]).astype(np.float64)
        if not (np.min(a) >= lo and np.max(a) <= hi): bad.append("range of " + k)
        elif np.any(a != np.floor(a)): bad.append("whole numbers in " + k)
    return bad
def lowest(n):
    same = n[:, :, :, None] == n[:, :, None, :]
    return ~np.any(same & np.tril(np.ones((L, L), bool), -1), axis=3)
def reference(xd, nx, pv, rc, ul, mv):
    X = np.ascontiguousarray(xd.astype(np.float32).astype(np.int32).reshape(N, 8, 16, W).transpose(0, 1, 3, 2))
    q = np.ascontiguousarray(mv.astype(np.float32).astype(np.int32).reshape(N, 8, 16, L).transpose(0, 1, 3, 2))
    nxt, pre, rec = nx.astype(np.int64), pv.astype(np.int64), rc.astype(np.int64)
    U = ul.astype(np.int64).reshape(N, 8, 16, V); v = np.zeros((N, 8, L), np.int64) + SV * np.arange(L)
    R3, G3 = np.arange(N)[:, None, None], np.arange(8)[None, :, None]; R4, G4 = R3[..., None], G3[..., None]
    for t in range(RO):
        d = np.take_along_axis(U, v[:, :, None, :], 3)
        score = np.add.reduce(np.abs(X[R4, G4, d] - q[:, :, None]), axis=4)
        cleared = np.zeros(d.shape, bool); c = d
        for f in range(F):
            c = nxt[R4, G4, c]
            cleared = cleared | (np.add.reduce((X[R4, G4, c] < q[:, :, None]).astype(np.int32), axis=4) >= TH)
        none = np.all(cleared, axis=2)
        k = np.where(none, np.argmax(score, axis=2), np.argmin(np.where(cleared, 2 ** 20, score), axis=2))
        a = np.take_along_axis(d, k[:, :, None, :], 2)[:, :, 0]; go = np.ones(a.shape, bool)
        for s in range(B):
            b = pre[R3, G3, a]
            go = go & (np.add.reduce((X[R3, G3, b] < q).astype(np.int32), axis=3) < TH)
            a = np.where(go, b, a)
        w = rec[R3, G3, a]
        A = np.add.reduce(none.reshape(N, -1).astype(np.int32), axis=1) & 255
        z = (q + A[:, None, None, None]) >> 1
        xn = (X[R3, G3, a] + q + 1) >> 1; nn = nxt[R3, G3, nxt[R3, G3, a]]
        r, g, i = np.nonzero(lowest(v)); U[r, g, k[r, g, i], v[r, g, i]] = a[r, g, i]
        r, g, i = np.nonzero(lowest(a)); X[r, g, a[r, g, i]] = xn[r, g, i]; nxt[r, g, a[r, g, i]] = nn[r, g, i]
        v = w + 0; q = z + 0
        for h in range(1, S):
            s = 1 + (t + h - 1) % (N - 1)
            v[:, :, h::S] = np.roll(w, s, axis=0)[:, :, h::S]; q[:, :, h::S] = np.roll(z, s, axis=0)[:, :, h::S]
    return {"yu": U.reshape(N, 128, V).astype(np.float32), "yx": np.ascontiguousarray(X.transpose(0, 1, 3, 2)).reshape(N, 128, W).astype(np.float32).astype(BF),
            "yv": v.astype(np.float32), "yq": np.ascontiguousarray(q.transpose(0, 1, 3, 2)).reshape(N, 128, L).astype(np.float32).astype(BF)}

@@ -1,0 +1,489 @@
+import numpy as np
+from concourse.bass import DstId, RemoteDMATransfer
+from concourse.mybir import dt, AluOpType as A, AxisListType, ActivationFunctionType as F
+
+SCRATCH = {}
+for _n, _c, _d in (
+        ("xt", 2304, "bfloat16"), ("x1", 2048, "bfloat16"), ("x2", 2048, "bfloat16"), ("x3", 2048, "bfloat16"),
+        ("x4", 2048, "bfloat16"), ("q16", 4096, "bfloat16"), ("qa", 256, "bfloat16"), ("qb", 256, "bfloat16"),
+        ("qo", 128, "bfloat16"), ("qr0", 128, "bfloat16"), ("qr1", 128, "bfloat16"), ("qr2", 128, "bfloat16"),
+        ("xg", 4096, "bfloat16"), ("ab", 4096, "bfloat16"), ("ca", 4096, "bfloat16"), ("cb", 4096, "bfloat16"),
+        ("xg4", 2048, "bfloat16"), ("sg4", 2048, "bfloat16"),
+        ("uw", 768, "float32"), ("ui", 512, "int32"), ("nxi", 2048, "int32"), ("nxr", 2304, "float32"),
+        ("pvr", 2048, "int32"), ("rcr", 2048, "int32"), ("idw", 2048, "float32"),
+        ("npi", 128, "int32"), ("npf", 128, "float32"), ("nxl", 128, "uint16"),
+        ("dd", 256, "float32"), ("d16", 256, "uint16"), ("vl", 16, "float32"), ("vl16", 16, "uint16"),
+        ("vn", 16, "float32"), ("vr", 256, "float32"), ("vx", 256, "float32"), ("yv1", 2176, "bfloat16"), ("ev", 2176, "bfloat16"),
+        ("ar", 256, "float16"), ("ar32", 256, "float32"), ("ax", 256, "float32"), ("ed", 256, "bfloat16"),
+        ("em", 1920, "bfloat16"), ("zz", 256, "bfloat16"),
+        ("dm", 256, "float32"), ("ds", 256, "float32"), ("lx", 16, "float32"),
+        ("vp16", 16, "uint16"), ("ap16", 16, "uint16"), ("m1", 256, "float32"), ("m2", 256, "float32"),
+        ("m3", 256, "float32"), ("th", 256, "float32"), ("lt", 256, "float32"), ("tk", 256, "float32"),
+        ("key", 256, "float32"), ("keyt", 256, "float32"), ("s1", 256, "float32"), ("eqt", 256, "float32"),
+        ("pd", 256, "float32"), ("s2", 256, "float16"), ("oh", 256, "float32"), ("fl", 16, "bfloat16"),
+        ("a016", 16, "uint16"), ("w1", 256, "float32"), ("sc1", 256, "float32"), ("w2", 256, "float32"),
+        ("sc2", 256, "float32"), ("bl", 32, "uint16"), ("xc", 512, "bfloat16"),
+        ("f1", 16, "float32"), ("d1", 16, "float32"), ("d2", 16, "float32"), ("f2", 16, "float32"), ("al", 16, "float32"),
+        ("al16", 16, "uint16"), ("w3", 256, "float32"), ("sc3", 256, "float32"), ("w4", 256, "float32"),
+        ("sc4", 256, "float32"), ("ws", 16, "float32"), ("we", 16, "float32"), ("wr0", 16, "float32"),
+        ("wr1", 16, "float32"), ("wr2", 16, "float32"), ("nl16", 16, "uint16"), ("nx2", 256, "float32"),
+        ("xga", 256, "bfloat16"), ("h1", 256, "float32"), ("xn", 256, "bfloat16"),
+        ("nj", 16, "float32"), ("cols", 64, "float32"), ("yy", 256, "float32"), ("y2", 256, "float32"),
+        ("ci", 64, "int32"), ("cf", 256, "float32"), ("cg", 128, "float32"), ("ch", 128, "float32"),
+        ("dg", 256, "float32"), ("dgt", 256, "float32"), ("dgu", 256, "float32"), ("tri", 256, "bfloat16"),
+        ("rst", 256, "float32"), ("zr", 256, "float32"), ("ek", 2048, "bfloat16"), ("cc", 128, "bfloat16"),
+        ("b4", 128, "bfloat16"), ("idf", 128, "float32"), ("idfn", 128, "float32"), ("idb", 128, "bfloat16"),
+        ("idn", 128, "bfloat16"), ("idh", 128, "float16"), ("sw", 512, "float16"), ("ones", 128, "bfloat16"),
+        ("exl", 16, "uint16"), ("exc", 16, "uint16"), ("sa", 4, "float32"), ("ra", 4, "float32")):
+    SCRATCH[_n] = ("sbuf", [128, _c], _d)
+for _k in range(8):
+    SCRATCH["p%d" % _k] = ("psum", [128, 512], "float32")
+
+ROUNDS = 3
+LS = 64
+XV = 1280
+SEMAPHORES = ["cv", "cs", "ct", "cp", "ldx", "ldq", "ldu", "ldn", "ldr", "ldp", "ldc", "nd0", "nd1", "out"]
+for _t in range(ROUNDS):
+    SEMAPHORES += ["%s%d" % (_a, _t) for _a in ("rq", "ra", "rw", "lq", "la", "lw")]
+BIG = 1048576.0
+MAG = 12582912.0
+
+
+def rank_program(g, core, T, topo):
+    rank = T.rank_of(core)
+    if rank is None:
+        return
+    N = len(T.cores)
+    V, S, P = g.vector, g.scalar, g.tensor
+    eng = {"v": V, "s": S, "t": P, "p": g, "y": g.sync}
+    own = {"v": "cv", "s": "cs", "t": "ct", "p": "cp"}
+    total = {}
+    known = {e: {} for e in eng}
+    clocks = {}
+    wr, rd, bank = {}, {}, {}
+
+    def need(e, deps):
+        for s in sorted(deps):
+            n = deps[s]
+            if known[e].get(s, 0) >= n:
+                continue
+            eng[e].wait_ge(T.sem[s], n)
+            for k, c in clocks.get((s, n), {}).items():
+                known[e][k] = max(known[e].get(k, 0), c)
+            known[e][s] = n
+
+    def deps_of(R, W, X, me):
+        d = {}
+
+        def put(s, n):
+            d[s] = max(d.get(s, 0), n)
+        for k in R:
+            if k in wr:
+                put(*wr[k])
+        for k in W:
+            if k in wr and wr[k][0] != me:
+                put(*wr[k])
+            for s, n in rd.get(k, {}).items():
+                if s != me:
+                    put(s, n)
+        for k in X:
+            for s, n in bank.get(k, {}).items():
+                if s != me:
+                    put(s, n)
+        return d
+
+    def note(s, n, R, W, X):
+        for k in R:
+            rd.setdefault(k, {})[s] = n
+        for k in W:
+            wr[k] = (s, n)
+            rd[k] = {}
+        for k in X:
+            bank.setdefault(k, {})[s] = n
+
+    def op(e, R, W, X, call):
+        me = own[e]
+        need(e, deps_of(R, W, X, me))
+        n = total.get(me, 0) + 1
+        total[me] = n
+        call().then_inc(T.sem[me], 1)
+        c = dict(known[e])
+        c[me] = n
+        clocks[(me, n)] = c
+        note(me, n, R, W, X)
+
+    def dma(e, sem, full, R, W, out, in_):
+        need(e, deps_of(R, W, [], sem))
+        total[sem] = total.get(sem, 0) + 16
+        eng[e].dma_start(out, in_).then_inc(T.sem[sem], 16)
+        c = dict(known[e])
+        c[sem] = full
+        clocks[(sem, full)] = c
+        note(sem, full, R, W, [])
+
+    def send(t, kind, src, key, dst, land):
+        d = T.cores[(rank + 1 + t % (N - 1)) % N]
+        es = topo.engines(core, d)[:8]
+        m = 0
+        for x in es:
+            m |= 1 << x
+        need("p", deps_of([key], [], [], None))
+        rid, pid = topo.addr(d, core)
+        rs, ls = "r" + kind + str(t), "l" + kind + str(t)
+        g.remote_dma(dst, src, T.sem[rs], T.sem[ls], pid, rid, m)
+        total[ls] = len(es)
+        note(ls, len(es), [key], [], [])
+        sender = T.cores[(rank - 1 - t % (N - 1)) % N]
+        total[rs] = len(topo.engines(sender, core)[:8])
+        wr[land] = (rs, total[rs])
+
+    def act(out, in_, R, W, X=(), func=F.Identity, **kw):
+        op("s", R, W, X, lambda: S.activation(out, in_, func, **kw))
+
+    def tt(out, a, b, o, R, W, X=()):
+        op("v", R, W, X, lambda: V.tensor_tensor(out, a, b, o))
+
+    def ts(out, a, s1, o1, R, W, X=(), s2=None, o2=None):
+        if o2 is None:
+            op("v", R, W, X, lambda: V.tensor_scalar(out, a, s1, None, o1))
+        else:
+            op("v", R, W, X, lambda: V.tensor_scalar(out, a, s1, s2, o1, o2))
+
+    def cp(out, in_, R, W, X=()):
+        op("v", R, W, X, lambda: V.tensor_copy(out, in_))
+
+    def vtr(out, in_, R, W, X=()):
+        op("v", R, W, X, lambda: V.transpose(out, in_))
+
+    def scan(out, d0, d1, o0, o1, R, W):
+        op("v", R, W, [], lambda: V.tensor_tensor_scan(out, d0, d1, 0.0, o0, o1))
+
+    def mm(out, l, r, st, sp, R, W, X):
+        op("t", R, W, X, lambda: P.matmul(out, l, r, st, sp))
+
+    def iota(out, pat, base, cm, W, whole=False):
+        if whole:
+            op("p", [], W, [], lambda: g.iota(out, pat, base, cm))
+        else:
+            op("p", [], W, [], lambda: g.iota(out, pat, base, cm, allow_small_or_imprecise_dtypes=True))
+
+    def col(j):
+        return T.cols[:, j:j + 1]
+
+    for b in range(8):
+        dma("y", "ldn", 128, [], ["npi"], T.npi[:, 16 * b:16 * b + 16], T.nx[b:b + 1, :])
+    dma("s", "ldu", 16, [], ["ui"], T.ui[:], T.ul[:])
+    dma("s", "ldx", 16, [], ["xt"], T.xt[:, 0:2048], T.xd[:])
+    dma("s", "ldq", 16, [], ["qa"], T.qa[:], T.mv[:])
+    for s, dst, src, k in (("ldr", T.nxi, T.nx, "nxi"), ("ldp", T.pvr, T.pv, "pvr"), ("ldc", T.rcr, T.rc, "rcr")):
+        for i in range(16):
+            dma("y", s, 256, ["xt", "ui", "qa"], [k], dst[i:128:16, :], src[:])
+    iota(T.ch[:], [[1, 128]], 0, -1, ["ch"])
+    iota(T.ci[:, 0:1], [[0, 1]], 0, 1, ["ci0"], True)
+    iota(T.cf[:], [[0, 16], [1, 16]], 0, 0, ["cf"])
+    iota(T.cg[:], [[1, 8], [0, 16]], 0, 0, ["cg"])
+    ts(T.idf[:], T.ch[:], 0.0, A.is_equal, ["ch"], ["idf"])
+    op("v", ["ci0"], ["ci3"], [], lambda: V.tensor_scalar(T.ci[:, 1:2], T.ci[:, 0:1], 15, None, A.bitwise_and))
+    op("v", ["ci0"], ["ci4"], [], lambda: V.tensor_scalar(T.ci[:, 2:3], T.ci[:, 0:1], 4, None, A.arith_shift_right))
+    op("v", ["ci0"], ["ci6"], [], lambda: V.tensor_scalar(T.ci[:, 4:5], T.ci[:, 0:1], 1, None, A.bitwise_and))
+    cp(col(0), T.ci[:, 1:2], ["ci3"], ["c0"])
+    cp(col(1), T.ci[:, 2:3], ["ci4"], ["c1"])
+    op("v", ["ci4"], ["ci5"], [], lambda: V.tensor_scalar(T.ci[:, 3:4], T.ci[:, 2:3], 1, None, A.bitwise_and))
+    cp(col(4), T.ci[:, 4:5], ["ci6"], ["c4"])
+    ts(T.idb[:], T.ch[:], 0.0, A.is_equal, ["ch"], ["idb"])
+    cp(col(2), T.ci[:, 3:4], ["ci5"], ["c2"])
+    ts(T.idn[:], T.ch[:], 0.0, A.is_equal, ["ch"], ["idn"], (), -1.0, A.mult)
+    ts(T.m1[:, 0:128], T.cg[:], col(1), A.is_equal, ["cg", "c1"], ["bs"])
+    ts(T.m1[:, 128:256], T.cf[:, 0:128], 1.0, A.add, ["cf"], ["cg2"])
+    tt(T.cc[:], T.m1[:, 0:128], T.m1[:, 128:256], A.mult, ["bs", "cg2"], ["cc"])
+    act(T.zr[:], T.cf[:], ["cf"], ["zr"], func=F.Sign)
+    act(T.rst[:], T.zr[:], ["zr"], ["rst"], scale=-2.0 * BIG, bias=BIG)
+    act(col(8), col(0), ["c0"], ["c8"], bias=0.5)
+    act(T.y2[:], T.cf[:], ["cf", "c8"], ["tri0"], scale=-1.0, bias=col(8), func=F.Sign)
+    act(T.tri[:], T.y2[:], ["tri0"], ["tri"], scale=4096.0, func=F.Relu)
+    act(T.qo[:], T.qa[:, 1::2], ["qa"], ["qo"])
+    send(0, "q", T.qo[:], "qo", T.qr0[:], "qr0")
+    iota(T.dgt[:], [[1, 256]], 2048, 0, ["dgt0"])
+    iota(T.dgu[:], [[1, 256]], 512, 0, ["dgu0"])
+    iota(T.ci[:, 16:32], [[16, 16]], 15, 0, ["ci1"], True)
+    iota(T.ci[:, 32:48], [[1, 16]], 0, 0, ["ci2"], True)
+    iota(T.nj[:], [[32, 16]], 0, 0, ["nj"])
+    iota(T.idw[:], [[1, 2048]], 0, 0, ["idw"])
+
+    def make_ek(ks):
+        for k in ks:
+            ts(T.ek[:, 128 * k:128 * k + 128], T.cc[:], float(k + 1), A.is_equal, ["cc"], ["ek"])
+
+    make_ek(range(8))
+    cp(T.d16[:], T.ui[:, 0:512:2], ["ui"], ["d16"])
+    cp(T.npf[:], T.npi[:], ["npi"], ["npf"])
+    mm(T.p7[:, 0:128], T.npf[:], T.idf[:], True, True, ["npf", "idf"], ["nxt"], ["p7"])
+    make_ek(range(8, 16))
+    cp(T.nxl[:], T.p7[:, 0:128], ["nxt"], ["nxl"], ["p7"])
+    cp(T.dd[:], T.ui[:, 0:512:2], ["ui"], ["dd"])
+
+    def first_fill():
+        for k in range(16):
+            cp(T.q16[:, k::16], T.qa[:], ["qa"], ["q16"])
+        vtr(T.p4[:, 0:256], T.dd[:], ["dd"], ["dt"], ["p4"])
+
+    def constants_on_scalar():
+        act(col(3), col(2), ["c2"], ["c3"], scale=-1.0, bias=1.0)
+        act(col(5), col(4), ["c4"], ["c5"], scale=-1.0, bias=1.0)
+        act(col(6), col(0), ["c0"], ["c6"], scale=2.0)
+        act(col(7), col(0), ["c0"], ["c7"], bias=65536.0)
+        act(T.idfn[:], T.idf[:], ["idf"], ["idfn"], scale=-1.0)
+        act(T.ones[:], T.cf[:, 0:128], ["cf"], ["ones"], scale=0.0, bias=1.0)
+        act(T.zz[:], T.cf[:], ["cf"], ["zz"], scale=0.0)
+
+    def constants_on_vector():
+        ts(T.dg[:], T.cf[:], col(0), A.is_equal, ["cf", "c0"], ["dg"])
+        ts(T.b4[:], T.cc[:], 0.0, A.is_gt, ["cc"], ["b4"], (), 4096.0, A.mult)
+        ts(T.idh[:], T.ch[:], 0.0, A.is_equal, ["ch"], ["idh"])
+        tt(T.dgt[:], T.dgt[:], T.dg[:], A.mult, ["dgt0", "dg"], ["dgt"])
+        tt(T.dgu[:], T.dgu[:], T.dg[:], A.mult, ["dgu0", "dg"], ["dgu"])
+        for j, (x, c) in enumerate(((0.0, 3), (16.0, 3), (-16.0, 2), (0.0, 2))):
+            ts(T.sw[:, 128 * j:128 * j + 128], T.ch[:], x, A.is_equal, ["ch", "c%d" % c], ["sw"], (), col(c), A.mult)
+        cp(T.exl[:], T.ci[:, 16:32], ["ci1"], ["exl"])
+        cp(T.exc[:], T.ci[:, 32:48], ["ci2"], ["exc"])
+        ts(T.vl[:], T.nj[:], col(6), A.add, ["nj", "c6"], ["vl"])
+        cp(T.vp16[:], T.vl[:], ["vl"], ["vp16"])
+        cp(T.uw[:, 0:512], T.ui[:], ["ui"], ["uw"])
+        cp(T.nxr[:, 0:2048], T.nxi[:], ["nxi"], ["nxr"])
+
+    def place_of(cnt, cb, pk, dgx, dk, al, alk, out16, outk):
+        tt(T.dm[:], cnt, dgx[:], A.min, [cb, dk], ["dm"], [pk])
+        scan(T.ds[:], T.zr[:], T.dm[:], A.mult, A.add, ["zr", "dm"], ["ds"])
+        tt(T.lx[:], T.ds[:, 15::16], al[:], A.max, ["ds", alk], ["lx"])
+        cp(out16[:], T.lx[:], ["lx"], [outk])
+
+    def sums(pout, src, keys, l0, l1, pk, dk):
+        for k in range(16):
+            mm(pout[:, l0:l1], T.ek[:, 128 * k:128 * k + 128], src(k), k == 0, k == 15, ["ek"] + keys, [dk], [pk])
+
+    SEG = [(0, 0)] * 15
+    _o = 0
+    for m in range(15):
+        SEG[m] = (_o, 240 - 16 * m)
+        _o += 240 - 16 * m
+
+    Q, QN, qk, qnk = T.qa, T.qb, "qa", "qb"
+    LV = 256 - LS
+    for t in range(ROUNDS):
+        last = t == ROUNDS - 1
+        xv = XV if t else 0
+
+        def walk(x, xk, out, ok, l0, l1):
+            tt(out[:, 16 * l0:16 * l1], x[:].indirect(T.d16[:, l0:l1]), T.q16[:, 16 * l0:16 * l1], A.is_lt,
+               xk + ["d16", "q16"], [ok + str(l0)])
+
+        def wsum(pout, out, ok, l0, l1, pk, dk):
+            sums(pout, lambda k: out[:, 16 * l0 + k:16 * l1:16], [ok + str(l0)], l0, l1, pk, dk + str(l0))
+
+        def diff(c, src, sk, lane0):
+            pk = ("p2", "p3")[c % 2]
+            j = 512 * c
+            mm(T[pk][:], T.idb[:], src[:, j:j + 512], True, False, ["idb", sk], [pk + "d"], [pk])
+            mm(T[pk][:], T.idn[:], T.q16[:, 16 * lane0 + j:16 * lane0 + j + 512], False, True, ["idn", "q16"], [pk + "d"], [pk])
+
+        def absc(c):
+            pk = ("p2", "p3")[c % 2]
+            act(T.ab[:, 512 * c:512 * c + 512], T[pk][:], [pk + "d"], ["ab%d" % (c // 4)], [pk], func=F.Abs)
+
+        def marks(l0, l1, k):
+            act(T.xg[:, 16 * l0:16 * l1], T.xt[:, 0:2048].indirect(T.d16[:, l0:l1]), ["xt", "d16"], [k])
+
+        if t:
+            cp(T.dd[:], T.uw[:, 0:512].indirect(T.vl16[:]), ["uw", "vl16"], ["dd"])
+            cp(T.d16[:], T.dd[:], ["dd"], ["d16"])
+            marks(0, 64, "xga0")
+            vtr(T.p4[:, 0:256], T.dd[:], ["dd"], ["dt"], ["p4"])
+            mm(T.p7[:, 0:128], T.npf[:], T.idf[:], True, True, ["npf", "idf"], ["nxt"], ["p7"])
+            cp(T.nxl[:], T.p7[:, 0:128], ["nxt"], ["nxl"], ["p7"])
+            cp(T.x1[:, 0:xv], T.xt[:, 0:2048].indirect(T.nxl[:, 0:xv // 16]), ["xt", "nxl"], ["x1a"])
+        else:
+            constants_on_scalar()
+            marks(0, 64, "xga0")
+        act(T.x1[:, xv:2048], T.xt[:, 0:2048].indirect(T.nxl[:, xv // 16:128]), ["xt", "nxl"], ["x1b"])
+        if t == 0:
+            first_fill()
+            constants_on_vector()
+        act(T.x2[:], T.x1[:].indirect(T.nxl[:]), ["x1a", "x1b", "nxl"], ["x2"])
+        walk(T.x1, ["x1a", "x1b"], T.ca, "ca", 0, 128)
+        marks(64, 128, "xgb0")
+        diff(0, T.xg, "xga0", 0)
+        diff(1, T.xg, "xga0", 0)
+        wsum(T.p0, T.ca, "ca", 0, 128, "p0", "k1")
+        walk(T.x1, ["x1a", "x1b"], T.ca, "ca", 128, 256)
+        absc(0)
+        absc(1)
+        diff(2, T.xg, "xgb0", 0)
+        diff(3, T.xg, "xgb0", 0)
+        absc(2)
+        absc(3)
+        wsum(T.p0, T.ca, "ca", 128, 256, "p0", "k1")
+        act(T.x3[:], T.x2[:].indirect(T.nxl[:]), ["x2", "nxl"], ["x3"])
+        act(T.m1[:], T.p0[:, 0:256], ["k10", "k1128"], ["m1"], ["p0"])
+        marks(128, 256, "xg1")
+        walk(T.x2, ["x2"], T.cb, "cb", 0, 128)
+        sums(T.p5, lambda k: T.ab[:, k:2048:16], ["ab0"], 0, 128, "p5", "sc0")
+        wsum(T.p1, T.cb, "cb", 0, 128, "p1", "k2")
+        walk(T.x2, ["x2"], T.cb, "cb", 128, 256)
+        diff(4, T.xg, "xg1", 0)
+        diff(5, T.xg, "xg1", 0)
+        absc(4)
+        absc(5)
+        diff(6, T.xg, "xg1", 0)
+        diff(7, T.xg, "xg1", 0)
+        absc(6)
+        absc(7)
+        wsum(T.p1, T.cb, "cb", 128, 256, "p1", "k2")
+        act(T.x4[:], T.x3[:].indirect(T.nxl[:]), ["x3", "nxl"], ["x4"])
+        walk(T.x3, ["x3"], T.ca, "ca", 0, 128)
+        sums(T.p5, lambda k: T.ab[:, 2048 + k::16], ["ab1"], 128, 256, "p5", "sc1")
+        wsum(T.p0, T.ca, "ca", 0, 128, "p0", "k3")
+        walk(T.x3, ["x3"], T.ca, "ca", 128, 256)
+        tt(T.m2[:], T.p1[:, 0:256], T.m1[:], A.max, ["k20", "k2128", "m1"], ["m2"], ["p1"])
+        wsum(T.p0, T.ca, "ca", 128, 256, "p0", "k3")
+        act(T.xg4[:, 0:16 * LS], T.x4[:].indirect(T.d16[:, LV:256]), ["x4", "d16"], ["xg4"])
+        act(T.p6[:, 0:256], T.p5[:, 0:256], ["sc0", "sc1"], ["amb"], ["p5", "p6"], scale=32.0, bias=-131072.0)
+        act(T.p6[:, 256:512], T.p5[:, 0:256], ["sc0", "sc1", "c7"], ["bb"], ["p5", "p6"], scale=-16.0, bias=col(7))
+        for c in range(LS // 32):
+            pk = ("p2", "p3")[c % 2]
+            diff(c, T.xg4, "xg4", LV)
+            act(T.sg4[:, 512 * c:512 * c + 512], T[pk][:], [pk + "d"], ["sg4"], [pk], func=F.Sign, bias=0.5)
+        walk(T.x4, ["x4"], T.cb, "cb", 0, 128)
+        wsum(T.p1, T.cb, "cb", 0, 128, "p1", "k4")
+        walk(T.x4, ["x4"], T.cb, "cb", 128, LV)
+        sums(T.p5, lambda k: T.sg4[:, k:16 * LS:16], ["sg4"], LV, 256, "p5", "k4s")
+        wsum(T.p1, T.cb, "cb", 128, LV, "p1", "k4")
+        tt(T.m3[:], T.p0[:, 0:256], T.m2[:], A.max, ["k30", "k3128", "m2"], ["m3"], ["p0"])
+        ts(T.th[:, 0:LV], T.m3[:, 0:LV], 9.0, A.is_lt, ["m3"], ["th0"], (), 9.0, A.mult)
+        ts(T.th[:, LV:256], T.m3[:, LV:256], 9.0, A.is_ge, ["m3"], ["th1"], (), 17.0, A.mult)
+        if t:
+            act(T.vn[:], T.vl[:], ["vl"], ["vn"], scale=-1.0)
+            act(T.vx[:], T.vl[:].indirect(T.exc[:]), ["vl", "exc"], ["vx"])
+            act(T.vr[:], T.idw[:].indirect(T.vl16[:]), ["idw", "vl16"], ["vr"])
+            mm(T.p3[:, 0:256], T.idfn[:], T.vx[:], True, False, ["idfn", "vx"], ["dv"], ["p3"])
+            mm(T.p3[:, 0:256], T.idf[:], T.vr[:], False, False, ["idf", "vr"], ["dv"], ["p3"])
+            mm(T.p3[:, 0:256], T.idb[:], T.tri[:], False, True, ["idb", "tri"], ["dv"], ["p3"])
+            for m, (o, n) in enumerate(SEG):
+                act(T.yv1[:, 256 + o:256 + o + n], T.vr[:, 256 - n:256], ["vr", "vn"], ["yv1"], func=F.Abs, bias=T.vn[:, m:m + 1])
+            act(T.yv1[:, 0:256], T.p3[:, 0:256], ["dv"], ["yv1"], ["p3"], func=F.Abs)
+            act(T.ev[:], T.yv1[:], ["yv1"], ["ev"], func=F.Relu, scale=-1.0, bias=1.0)
+        tt(T.lt[:, LV:256], T.p5[:, LV:256], T.th[:, LV:256], A.is_ge, ["k4s", "th1"], ["lt1"], ["p5"])
+        tt(T.lt[:, 0:LV], T.p1[:, 0:LV], T.th[:, 0:LV], A.is_lt, ["k40", "k4128", "th0"], ["lt0"], ["p1"])
+        tt(T.tk[:], T.p6[:, 0:256], T.lt[:], A.mult, ["amb", "lt0", "lt1"], ["tk"], ["p6"])
+        tt(T.key[:], T.p6[:, 256:512], T.tk[:], A.add, ["bb", "tk"], ["key"], ["p6"])
+        vtr(T.keyt[:], T.key[:], ["key"], ["keyt"])
+        scan(T.s1[:], T.rst[:], T.keyt[:], A.max, A.min, ["rst", "keyt"], ["s1"])
+        tt(T.eqt[:], T.s1[:].indirect(T.exl[:]), T.keyt[:], A.is_equal, ["s1", "exl", "keyt"], ["eqt"])
+        tt(T.pd[:], T.p4[:, 0:256], T.eqt[:], A.mult, ["dt", "eqt"], ["pd"], ["p4"])
+        scan(T.s2[:], T.zr[:], T.pd[:], A.mult, A.add, ["zr", "pd"], ["s2"])
+        for e in (0, 1):
+            for h in (0, 1):
+                mm(T.p7[:, e:16:2], T.sw[:, 128 * (2 * e + h):128 * (2 * e + h) + 128], T.s2[:, 15 + 16 * h::32], h == 0, h == 1,
+                   ["sw", "s2"], ["a0"], ["p7"])
+        ts(T.fl[:], T.s1[:, 15::16], 0.0, A.is_ge, ["s1"], ["fl"])
+        vtr(T.oh[:], T.eqt[:], ["eqt"], ["oh"])
+        cp(T.a016[:], T.p7[:, 0:16], ["a0"], ["a016"], ["p7"])
+        mm(T.p7[:, 32:48], T.ones[:], T.fl[:], True, True, ["ones", "fl"], ["nn"], ["p7"])
+        sa, ra = T.sa[:, t:t + 1], T.ra[:, t:t + 1]
+        act(T.nj[:], T.p7[:, 32:48], ["nn"], ["nj", "n"], ["p7"], accum_out=col(16))
+        act(col(17), col(16), ["n"], ["n1"], scale=1.0 / 256, bias=-0.498046875)
+        act(col(20), col(16), ["n"], ["n4"], scale=0.5, bias=-0.25)
+        act(col(18), col(17), ["n1"], ["n2"], bias=MAG)
+        act(col(19), col(18), ["n2"], ["n3"], bias=-MAG)
+        act(sa, col(19), ["n3", "n4"], ["sa%d" % t], scale=-128.0, bias=col(20))
+        send(t, "a", sa, "sa%d" % t, ra, "ra%d" % t)
+        tt(T.w1[:], T.pvr[:].indirect(T.a016[:]), T.dg[:], A.mult, ["pvr", "a016", "dg"], ["w1"])
+        scan(T.sc1[:], T.zr[:], T.w1[:], A.mult, A.add, ["zr", "w1"], ["sc1"])
+        cp(T.bl[:, 0:16], T.sc1[:, 15::16], ["sc1"], ["bl0"])
+        tt(T.w2[:], T.pvr[:].indirect(T.bl[:, 0:16]), T.dg[:], A.mult, ["pvr", "bl0", "dg"], ["w2"])
+        tt(T.xc[:, 0:256], T.xt[:, 0:2048].indirect(T.bl[:, 0:16]), Q[:], A.is_lt, ["xt", "bl0", qk], ["xc0"])
+        sums(T.p7, lambda k: T.xc[:, k:256:16], ["xc0"], 16, 32, "p7", "b1")
+        scan(T.sc2[:], T.zr[:], T.w2[:], A.mult, A.add, ["zr", "w2"], ["sc2"])
+        cp(T.bl[:, 16:32], T.sc2[:, 15::16], ["sc2"], ["bl1"])
+        tt(T.xc[:, 256:512], T.xt[:, 0:2048].indirect(T.bl[:, 16:32]), Q[:], A.is_lt, ["xt", "bl1", qk], ["xc1"])
+        sums(T.p0, lambda k: T.xc[:, 256 + k::16], ["xc1"], 0, 16, "p0", "b2")
+        mm(T.p5[:, 0:256], T.b4[:], T.zz[:], True, False, ["b4", "zz"], ["ca_"], ["p5"])
+        mm(T.p3[:, 0:256], T.idb[:], T.tri[:], True, False, ["idb", "tri"], ["da"], ["p3"])
+        mm(T.p1[:, 256:512], T.idb[:], Q[:], True, False, ["idb", qk], ["xq"], ["p1"])
+        mm(T.p6[:, 0:256], T.idfn[:], T.dd[:], True, False, ["idfn", "dd"], ["ad"], ["p6"])
+        tt(T.d1[:], T.sc1[:, 15::16], T.p7[:, 0:16], A.subtract, ["sc1", "a0"], ["d1"], ["p7"])
+        ts(T.f1[:], T.p7[:, 16:32], 9.0, A.is_lt, ["b1"], ["f1"], ["p7"])
+        tt(T.d2[:], T.sc2[:, 15::16], T.sc1[:, 15::16], A.subtract, ["sc1", "sc2"], ["d2"])
+        tt(T.d1[:], T.d1[:], T.f1[:], A.mult, ["d1", "f1"], ["d1"])
+        tt(T.d2[:], T.d2[:], T.f1[:], A.mult, ["d2", "f1"], ["d2"])
+        tt(T.d1[:], T.d1[:], T.p7[:, 0:16], A.add, ["d1", "a0"], ["d1"], ["p7"])
+        ts(T.f2[:], T.p0[:, 0:16], 9.0, A.is_lt, ["b2"], ["f2"], ["p0"])
+        tt(T.f2[:], T.f2[:], T.d2[:], A.mult, ["f2", "d2"], ["f2"])
+        tt(T.al[:], T.f2[:], T.d1[:], A.add, ["f2", "d1"], ["al"])
+        cp(T.al16[:], T.al[:], ["al"], ["al16"])
+        tt(T.w3[:], T.rcr[:].indirect(T.al16[:]), T.dg[:], A.mult, ["rcr", "al16", "dg"], ["w3"])
+        act(T.ar32[:], T.idw[:].indirect(T.al16[:]), ["idw", "al16"], ["ar32"])
+        act(T.ax[:], T.al[:].indirect(T.exc[:]), ["al", "exc"], ["ax"])
+        act(T.xga[:], T.xt[:, 0:2048].indirect(T.al16[:]), ["xt", "al16"], ["xga"])
+        if not last:
+            tt(T.w4[:], T.nxr[:, 0:2048].indirect(T.al16[:]), T.dg[:], A.mult, ["nxr", "al16", "dg"], ["w4"])
+        scan(T.sc3[:], T.zr[:], T.w3[:], A.mult, A.add, ["zr", "w3"], ["sc3"])
+        if not last:
+            scan(T.sc4[:], T.zr[:], T.w4[:], A.mult, A.add, ["zr", "w4"], ["sc4"])
+        ts(T.ws[:], T.sc3[:, 15::16], col(4), A.mult, ["sc3", "c4"], ["ws"])
+        wrt, wk = T["wr%d" % t], "wr%d" % t
+        send(t, "w", T.ws[:], "ws", wrt[:], wk)
+        if not last:
+            cp(T.nl16[:], T.sc4[:, 15::16], ["sc4"], ["nl16"])
+        cp(T.ar[:], T.ar32[:], ["ar32"], ["ar"])
+        ts(T.we[:], T.sc3[:, 15::16], col(5), A.mult, ["sc3", "c5"], ["we"])
+        mm(T.p3[:, 0:256], T.idfn[:], T.ax[:], False, False, ["idfn", "ax"], ["da"], ["p3"])
+        mm(T.p1[:, 256:512], T.idb[:], T.xga[:], False, True, ["idb", "xga"], ["xq"], ["p1"])
+        mm(T.p3[:, 0:256], T.idh[:], T.ar[:], False, True, ["idh", "ar"], ["da"], ["p3"])
+        mm(T.p6[:, 0:256], T.idh[:], T.ar[:], False, True, ["idh", "ar"], ["ad"], ["p6"])
+        if not last:
+            act(T.nx2[:], T.nxr[:, 0:2048].indirect(T.nl16[:]), ["nxr", "nl16"], ["nx2"])
+        act(T.h1[:], T.p1[:, 256:512], ["xq"], ["h1"], ["p1"], scale=0.5, bias=0.25)
+        qrt = T["qr%d" % t]
+        act(T.yy[:, 0::2], Q[:, 0::2], [qk, "sa%d" % t], ["yy0"], scale=0.5, bias=sa)
+        act(T.h1[:], T.h1[:], ["h1"], ["h2"], bias=MAG)
+        act(T.yy[:, 1::2], qrt[:], ["qr%d" % t, "ra%d" % t], ["yy1"], scale=0.5, bias=ra)
+        act(T.xn[:], T.h1[:], ["h2"], ["xn"], bias=-MAG)
+        act(T.y2[:], T.yy[:], ["yy0", "yy1"], ["y2"], bias=MAG)
+        act(QN[:], T.y2[:], ["y2"], [qnk], bias=-MAG)
+        if not last:
+            act(T.qo[:], QN[:, 1::2], [qnk], ["qo"])
+            send(t + 1, "q", T.qo[:], "qo", T["qr%d" % (t + 1)][:], "qr%d" % (t + 1))
+            for k in range(16):
+                act(T.q16[:, k::16], T.y2[:], ["y2"], ["q16"], bias=-MAG)
+        else:
+            dma("y", "out", 64, [qnk], ["yq"], T.yq[:], QN[:])
+        for m, (o, n) in enumerate(SEG):
+            ts(T.em[:, o:o + n], T.ar[:, 256 - n:256], T.al[:, m:m + 1], A.is_equal, ["ar", "al"], ["em%d" % m])
+            mm(T.p5[:, 256 - n:256], T.b4[:], T.em[:, o:o + n], False, False, ["b4", "em%d" % m], ["ca_"], ["p5"])
+        ts(T.ed[:], T.p3[:, 0:256], 0.0, A.is_equal, ["da"], ["ed"], ["p3"])
+        mm(T.p5[:, 0:256], T.b4[:], T.ed[:], False, True, ["b4", "ed"], ["ca_"], ["p5"])
+        tt(T.tk[:], T.p6[:, 0:256], T.oh[:], A.mult, ["ad", "oh"], ["ut"], ["p6"])
+        if t:
+            for m, (o, n) in enumerate([(-256, 256)] + SEG):
+                mm(T.p2[:, 256 - n:256], T.b4[:], T.ev[:, 256 + o:256 + o + n], m == 0, m == 15, ["b4", "ev"], ["cv_"], ["p2"])
+        place_of(T.p5[:, 0:256], "ca_", "p5", T.dgt, "dgt", T.al, "al", T.ap16, "ap16")
+        if not last:
+            cp(T.nxr[:].indirect(T.ap16[:]), T.nx2[:], ["nx2", "ap16"], ["nxr"])
+            for b in range(8):
+                dma("y", "nd%d" % t, 128, ["nxr"], ["npf"], T.npf[:, 16 * b:16 * b + 16], T.nxr[16 * b:16 * b + 1, 0:2048])
+        cp(T.xt[:].indirect(T.ap16[:]), T.xn[:], ["xn", "ap16"], ["xt"])
+        if last:
+            dma("y", "out", 64, ["xt"], ["yx"], T.yx[:], T.xt[:, 0:2048])
+        if t:
+            place_of(T.p2[:, 0:256], "cv_", "p2", T.dgu, "dgu", T.vl, "vl", T.vp16, "vp16")
+        tt(T.vl[:], T.we[:], wrt[:], A.add, ["we", wk], ["vl"])
+        cp(T.vl16[:], T.vl[:], ["vl"], ["vl16"])
+        tt(T.uw[:].indirect(T.vp16[:]), T.tk[:], T.dd[:], A.add, ["ut", "dd", "vp16"], ["uw"])
+        if last:
+            dma("y", "out", 64, ["uw"], ["yu"], T.yu[:], T.uw[:, 0:512])
+        Q, QN, qk, qnk = QN, Q, qnk, qk
+    act(T.vr[:], T.idw[:].indirect(T.vl16[:]), ["idw", "vl16"], ["vr"])
+    dma("y", "out", 64, ["vr"], ["yv"], T.yv[:], T.vr[0:128:16, :])
+    for s in SEMAPHORES:
+        if total.get(s, 0) > known["p"].get(s, 0):
+            g.wait_ge(T.sem[s], total[s])

@@ -9,7 +9,7 @@ for _n, _c, _d in (
         ("qo", 128, "bfloat16"), ("qr0", 128, "bfloat16"), ("qr1", 128, "bfloat16"), ("qr2", 128, "bfloat16"),
         ("xg", 4096, "bfloat16"), ("ab", 4096, "bfloat16"), ("ca", 4096, "bfloat16"), ("cb", 4096, "bfloat16"),
         ("xg4", 2048, "bfloat16"), ("sg4", 2048, "bfloat16"),
-        ("uw", 768, "float32"), ("ui", 512, "int32"), ("nxi", 2048, "int32"), ("nxr", 2304, "float32"),
+        ("uw", 768, "float32"), ("ui", 512, "int32"), ("i16", 128, "bfloat16"), ("i32", 128, "bfloat16"), ("k8", 128, "bfloat16"), ("kk1", 128, "bfloat16"), ("nxr", 2304, "float32"),
         ("pvr", 2048, "int32"), ("rcr", 2048, "int32"), ("idw", 2048, "float32"),
         ("npi", 128, "int32"), ("npf", 128, "float32"), ("nxl", 128, "uint16"),
         ("dd", 256, "float32"), ("d16", 256, "uint16"), ("vl", 16, "float32"), ("vl16", 16, "uint16"),
@@ -17,8 +17,8 @@ for _n, _c, _d in (
         ("ar", 256, "float16"), ("ar32", 256, "float32"), ("ax", 256, "float32"), ("ed", 256, "bfloat16"),
         ("em", 1920, "bfloat16"), ("zz", 256, "bfloat16"),
         ("dm", 256, "float32"), ("ds", 256, "float32"), ("lx", 16, "float32"),
-        ("vp16", 16, "uint16"), ("ap16", 16, "uint16"), ("m1", 256, "float32"), ("m2", 256, "float32"),
-        ("m3", 256, "float32"), ("th", 256, "float32"), ("lt", 256, "float32"), ("tk", 256, "float32"),
+        ("vp16", 16, "uint16"), ("ap16", 16, "uint16"), ("m1", 256, "float32"), ("nph", 128, "float16"), ("npt", 128, "float16"),
+        ("rr", 768, "bfloat16"), ("tk", 256, "float32"),
         ("key", 256, "float32"), ("keyt", 256, "float32"), ("s1", 256, "float32"), ("eqt", 256, "float32"),
         ("pd", 256, "float32"), ("s2", 256, "float16"), ("oh", 256, "float32"), ("fl", 16, "bfloat16"),
         ("a016", 16, "uint16"), ("w1", 256, "float32"), ("sc1", 256, "float32"), ("w2", 256, "float32"),
@@ -35,16 +35,24 @@ for _n, _c, _d in (
         ("b4", 128, "bfloat16"), ("idf", 128, "float32"), ("idfn", 128, "float32"), ("idb", 128, "bfloat16"),
         ("idn", 128, "bfloat16"), ("idh", 128, "float16"), ("sw", 512, "float16"), ("ones", 128, "bfloat16"),
         ("exl", 16, "uint16"), ("exc", 16, "uint16"), ("sa", 4, "float32"), ("ra", 4, "float32")):
-    SCRATCH[_n] = ("sbuf", [128, _c], _d)
+    _d = {"w1": "float16", "w2": "float16", "w3": "float16", "w4": "float16", "sc1": "float16", "sc2": "float16",
+          "sc3": "float16", "sc4": "float16", "dm": "float16", "ds": "float16", "pd": "float16",
+          "zr": "bfloat16", "eqt": "bfloat16", "oh": "bfloat16"}.get(_n, _d)
+    SCRATCH[_n] = ("sbuf", [128, 2560 if _c == 2304 else _c], _d)
 for _k in range(8):
     SCRATCH["p%d" % _k] = ("psum", [128, 512], "float32")
 
+SCRATCH["nxd"] = ("dram", [8, 2048], "float32")
+
 ROUNDS = 3
-LS = 64
-XV = 1280
-SEMAPHORES = ["cv", "cs", "ct", "cp", "ldx", "ldq", "ldu", "ldn", "ldr", "ldp", "ldc", "nd0", "nd1", "out"]
+LSS = (64, 64, 64)
+XV0, XV = 512, 1024
+SEMAPHORES = ["cv", "cs", "ct", "cp", "ldx", "ldq", "ldu", "ldn", "ldr", "ldd", "ldp", "ldc", "nd0", "nd1", "out"]
 for _t in range(ROUNDS):
     SEMAPHORES += ["%s%d" % (_a, _t) for _a in ("rq", "ra", "rw", "lq", "la", "lw")]
+GK0, GK = 4, 8
+VM = 0
+FAR = 262144.0
 BIG = 1048576.0
 MAG = 12582912.0
 
@@ -170,14 +178,19 @@ def rank_program(g, core, T, topo):
     def col(j):
         return T.cols[:, j:j + 1]
 
-    for b in range(8):
-        dma("y", "ldn", 128, [], ["npi"], T.npi[:, 16 * b:16 * b + 16], T.nx[b:b + 1, :])
-    dma("s", "ldu", 16, [], ["ui"], T.ui[:], T.ul[:])
-    dma("s", "ldx", 16, [], ["xt"], T.xt[:, 0:2048], T.xd[:])
+    dma("y", "ldn", 16, [], ["npi"], T.npi[:], T.nx[:])
+    dma("y", "ldx", 16, [], ["xt"], T.xt[:, 0:2048], T.xd[:])
     dma("s", "ldq", 16, [], ["qa"], T.qa[:], T.mv[:])
-    for s, dst, src, k in (("ldr", T.nxi, T.nx, "nxi"), ("ldp", T.pvr, T.pv, "pvr"), ("ldc", T.rcr, T.rc, "rcr")):
+    dma("s", "ldu", 16, [], ["ui"], T.ui[:], T.ul[:])
+    for s, dst, src, k in (("ldp", T.pvr, T.pv, "pvr"), ("ldc", T.rcr, T.rc, "rcr")):
         for i in range(16):
             dma("y", s, 256, ["xt", "ui", "qa"], [k], dst[i:128:16, :], src[:])
+
+    def repeat_nx():
+        dma("y", "ldd", 16, ["npf"], ["nxd"], T.nxd[:], T.npf[:])
+        for i in range(16):
+            dma("y", "ldr", 256, ["nxd"], ["nxr"], T.nxr[i:128:16, 0:2048], T.nxd[:])
+
     iota(T.ch[:], [[1, 128]], 0, -1, ["ch"])
     iota(T.ci[:, 0:1], [[0, 1]], 0, 1, ["ci0"], True)
     iota(T.cf[:], [[0, 16], [1, 16]], 0, 0, ["cf"])
@@ -192,6 +205,7 @@ def rank_program(g, core, T, topo):
     cp(col(4), T.ci[:, 4:5], ["ci6"], ["c4"])
     ts(T.idb[:], T.ch[:], 0.0, A.is_equal, ["ch"], ["idb"])
     cp(col(2), T.ci[:, 3:4], ["ci5"], ["c2"])
+    ts(col(3), T.ci[:, 3:4], 0.0, A.is_equal, ["ci5"], ["c3"])
     ts(T.idn[:], T.ch[:], 0.0, A.is_equal, ["ch"], ["idn"], (), -1.0, A.mult)
     ts(T.m1[:, 0:128], T.cg[:], col(1), A.is_equal, ["cg", "c1"], ["bs"])
     ts(T.m1[:, 128:256], T.cf[:, 0:128], 1.0, A.add, ["cf"], ["cg2"])
@@ -203,59 +217,92 @@ def rank_program(g, core, T, topo):
     act(T.tri[:], T.y2[:], ["tri0"], ["tri"], scale=4096.0, func=F.Relu)
     act(T.qo[:], T.qa[:, 1::2], ["qa"], ["qo"])
     send(0, "q", T.qo[:], "qo", T.qr0[:], "qr0")
-    iota(T.dgt[:], [[1, 256]], 2048, 0, ["dgt0"])
-    iota(T.dgu[:], [[1, 256]], 512, 0, ["dgu0"])
+
+    def repeat_q(ks, q, qk):
+        for k in ks:
+            op("p", [qk], ["q16g"], [], lambda: g.affine_select(T.q16[:, k::16], q[:], [[0, 256]], A.is_gt, 0.0, 1, 0))
+
+    repeat_q(range(16 - GK0, 16), T.qa, "qa")
     iota(T.ci[:, 16:32], [[16, 16]], 15, 0, ["ci1"], True)
     iota(T.ci[:, 32:48], [[1, 16]], 0, 0, ["ci2"], True)
     iota(T.nj[:], [[32, 16]], 0, 0, ["nj"])
+    iota(T.dgt[:], [[2, 256]], 2048, 0, ["dgt0"])
+    iota(T.dgu[:], [[1, 256]], 512, 0, ["dgu0"])
     iota(T.idw[:], [[1, 2048]], 0, 0, ["idw"])
 
     def make_ek(ks):
         for k in ks:
-            ts(T.ek[:, 128 * k:128 * k + 128], T.cc[:], float(k + 1), A.is_equal, ["cc"], ["ek"])
+            ts(T.ek[:, 128 * k:128 * k + 128], T.cc[:], float(k + 1), A.is_equal, ["cc"], ["ek"], (), FAR, A.mult)
 
     make_ek(range(8))
     cp(T.d16[:], T.ui[:, 0:512:2], ["ui"], ["d16"])
+    cp(T.nph[:], T.npi[:], ["npi"], ["nph"])
     cp(T.npf[:], T.npi[:], ["npi"], ["npf"])
-    mm(T.p7[:, 0:128], T.npf[:], T.idf[:], True, True, ["npf", "idf"], ["nxt"], ["p7"])
+    repeat_nx()
+
+    def list_of_nx():
+        vtr(T.npt[:], T.nph[:], ["nph"], ["npt"])
+        for e in (0, 1):
+            for b in range(4):
+                for h in (0, 1):
+                    mm(T.p7[:, 2 * b + e:128:8], T.sw[:, 128 * (2 * e + h):128 * (2 * e + h) + 128],
+                       T.npt[:, 32 * b + 16 * h:32 * b + 16 * h + 16], h == 0, h == 1, ["sw", "npt"], ["nxt"], ["p7"])
+
+    for j, (x, c) in enumerate(((0.0, 3), (16.0, 3), (-16.0, 2), (0.0, 2))):
+        ts(T.sw[:, 128 * j:128 * j + 128], T.ch[:], x, A.is_equal, ["ch", "c%d" % c], ["sw"], (), col(c), A.mult)
+    list_of_nx()
     make_ek(range(8, 16))
     cp(T.nxl[:], T.p7[:, 0:128], ["nxt"], ["nxl"], ["p7"])
     cp(T.dd[:], T.ui[:, 0:512:2], ["ui"], ["dd"])
 
     def first_fill():
-        for k in range(16):
+        for k in range(16 - GK0):
             cp(T.q16[:, k::16], T.qa[:], ["qa"], ["q16"])
         vtr(T.p4[:, 0:256], T.dd[:], ["dd"], ["dt"], ["p4"])
 
     def constants_on_scalar():
-        act(col(3), col(2), ["c2"], ["c3"], scale=-1.0, bias=1.0)
         act(col(5), col(4), ["c4"], ["c5"], scale=-1.0, bias=1.0)
         act(col(6), col(0), ["c0"], ["c6"], scale=2.0)
         act(col(7), col(0), ["c0"], ["c7"], bias=65536.0)
+        act(col(9), col(0), ["c0"], ["c9"], bias=-65536.0)
+        for w, k, x in ((T.i16, "i16", 16.0), (T.i32, "i32", 32.0), (T.k8, "k8", -8.4 * FAR), (T.kk1, "kk1", -FAR)):
+            act(w[:], T.idb[:], ["idb"], [k], scale=x)
         act(T.idfn[:], T.idf[:], ["idf"], ["idfn"], scale=-1.0)
         act(T.ones[:], T.cf[:, 0:128], ["cf"], ["ones"], scale=0.0, bias=1.0)
         act(T.zz[:], T.cf[:], ["cf"], ["zz"], scale=0.0)
 
     def constants_on_vector():
         ts(T.dg[:], T.cf[:], col(0), A.is_equal, ["cf", "c0"], ["dg"])
+
+    def later_constants():
         ts(T.b4[:], T.cc[:], 0.0, A.is_gt, ["cc"], ["b4"], (), 4096.0, A.mult)
         ts(T.idh[:], T.ch[:], 0.0, A.is_equal, ["ch"], ["idh"])
-        tt(T.dgt[:], T.dgt[:], T.dg[:], A.mult, ["dgt0", "dg"], ["dgt"])
-        tt(T.dgu[:], T.dgu[:], T.dg[:], A.mult, ["dgu0", "dg"], ["dgu"])
-        for j, (x, c) in enumerate(((0.0, 3), (16.0, 3), (-16.0, 2), (0.0, 2))):
-            ts(T.sw[:, 128 * j:128 * j + 128], T.ch[:], x, A.is_equal, ["ch", "c%d" % c], ["sw"], (), col(c), A.mult)
         cp(T.exl[:], T.ci[:, 16:32], ["ci1"], ["exl"])
         cp(T.exc[:], T.ci[:, 32:48], ["ci2"], ["exc"])
         ts(T.vl[:], T.nj[:], col(6), A.add, ["nj", "c6"], ["vl"])
         cp(T.vp16[:], T.vl[:], ["vl"], ["vp16"])
         cp(T.uw[:, 0:512], T.ui[:], ["ui"], ["uw"])
-        cp(T.nxr[:, 0:2048], T.nxi[:], ["nxi"], ["nxr"])
 
-    def place_of(cnt, cb, pk, dgx, dk, al, alk, out16, outk):
-        tt(T.dm[:], cnt, dgx[:], A.min, [cb, dk], ["dm"], [pk])
-        scan(T.ds[:], T.zr[:], T.dm[:], A.mult, A.add, ["zr", "dm"], ["ds"])
-        tt(T.lx[:], T.ds[:, 15::16], al[:], A.max, ["ds", alk], ["lx"])
-        cp(out16[:], T.lx[:], ["lx"], [outk])
+    def places_past_the_end(step):
+        if step == 0:
+            act(T.yy[:], T.dg[:], ["dg"], ["dgs"], scale=4096.0, bias=-4096.0)
+        for w, k, pb in ((T.dgt, "dgt", "p4"), (T.dgu, "dgu", "p5")):
+            pw = T[pb][:, 256:512]
+            if step == 0:
+                mm(pw, T.idf[:], w[:], True, False, ["idf", k + "0"], [k + "p"], [pb])
+                mm(pw, T.idf[:], T.yy[:], False, True, ["idf", "dgs"], [k + "p"], [pb])
+            else:
+                act(w[:], pw, [k + "p"], [k], [pb], func=F.Relu)
+
+    def places(jobs):
+        for cb, pk, dgx, dk, al, alk, out16, outk, (dm, ds, lx) in jobs:
+            tt(dm[:], T[pk][:, 0:256], dgx[:], A.min, [cb, dk], ["dm" + pk], [pk])
+        for cb, pk, dgx, dk, al, alk, out16, outk, (dm, ds, lx) in jobs:
+            scan(ds[:], T.zr[:], dm[:], A.mult, A.add, ["zr", "dm" + pk], ["ds" + pk])
+        for cb, pk, dgx, dk, al, alk, out16, outk, (dm, ds, lx) in jobs:
+            tt(lx[:], ds[:, 15::16], al[:], A.max, ["ds" + pk, alk], ["lx" + pk])
+        for cb, pk, dgx, dk, al, alk, out16, outk, (dm, ds, lx) in jobs:
+            cp(out16[:], lx[:], ["lx" + pk], [outk])
 
     def sums(pout, src, keys, l0, l1, pk, dk):
         for k in range(16):
@@ -268,14 +315,15 @@ def rank_program(g, core, T, topo):
         _o += 240 - 16 * m
 
     Q, QN, qk, qnk = T.qa, T.qb, "qa", "qb"
-    LV = 256 - LS
     for t in range(ROUNDS):
         last = t == ROUNDS - 1
-        xv = XV if t else 0
+        LS = LSS[t]
+        LV = 256 - LS
+        xv = XV if t else XV0
 
         def walk(x, xk, out, ok, l0, l1):
             tt(out[:, 16 * l0:16 * l1], x[:].indirect(T.d16[:, l0:l1]), T.q16[:, 16 * l0:16 * l1], A.is_lt,
-               xk + ["d16", "q16"], [ok + str(l0)])
+               xk + ["d16", "q16", "q16g"], [ok + str(l0)])
 
         def wsum(pout, out, ok, l0, l1, pk, dk):
             sums(pout, lambda k: out[:, 16 * l0 + k:16 * l1:16], [ok + str(l0)], l0, l1, pk, dk + str(l0))
@@ -284,7 +332,7 @@ def rank_program(g, core, T, topo):
             pk = ("p2", "p3")[c % 2]
             j = 512 * c
             mm(T[pk][:], T.idb[:], src[:, j:j + 512], True, False, ["idb", sk], [pk + "d"], [pk])
-            mm(T[pk][:], T.idn[:], T.q16[:, 16 * lane0 + j:16 * lane0 + j + 512], False, True, ["idn", "q16"], [pk + "d"], [pk])
+            mm(T[pk][:], T.idn[:], T.q16[:, 16 * lane0 + j:16 * lane0 + j + 512], False, True, ["idn", "q16", "q16g"], [pk + "d"], [pk])
 
         def absc(c):
             pk = ("p2", "p3")[c % 2]
@@ -294,24 +342,29 @@ def rank_program(g, core, T, topo):
             act(T.xg[:, 16 * l0:16 * l1], T.xt[:, 0:2048].indirect(T.d16[:, l0:l1]), ["xt", "d16"], [k])
 
         if t:
-            cp(T.dd[:], T.uw[:, 0:512].indirect(T.vl16[:]), ["uw", "vl16"], ["dd"])
-            cp(T.d16[:], T.dd[:], ["dd"], ["d16"])
-            marks(0, 64, "xga0")
+            cp(T.d16[:], T.uw[:, 0:512].indirect(T.vl16[:]), ["uw", "vl16"], ["d16"])
+            act(T.dd[:], T.uw[:, 0:512].indirect(T.vl16[:]), ["uw", "vl16"], ["dd"])
+            marks(VM, 64, "xga0")
             vtr(T.p4[:, 0:256], T.dd[:], ["dd"], ["dt"], ["p4"])
-            mm(T.p7[:, 0:128], T.npf[:], T.idf[:], True, True, ["npf", "idf"], ["nxt"], ["p7"])
+            if VM:
+                cp(T.xg[:, 0:16 * VM], T.xt[:, 0:2048].indirect(T.d16[:, 0:VM]), ["xt", "d16"], ["xgv"])
+            cp(T.nph[:], T.npf[:], ["npf"], ["nph"])
+            list_of_nx()
             cp(T.nxl[:], T.p7[:, 0:128], ["nxt"], ["nxl"], ["p7"])
             cp(T.x1[:, 0:xv], T.xt[:, 0:2048].indirect(T.nxl[:, 0:xv // 16]), ["xt", "nxl"], ["x1a"])
         else:
             constants_on_scalar()
-            marks(0, 64, "xga0")
         act(T.x1[:, xv:2048], T.xt[:, 0:2048].indirect(T.nxl[:, xv // 16:128]), ["xt", "nxl"], ["x1b"])
         if t == 0:
+            marks(0, 64, "xga0")
             first_fill()
+            cp(T.x1[:, 0:xv], T.xt[:, 0:2048].indirect(T.nxl[:, 0:xv // 16]), ["xt", "nxl"], ["x1a"])
             constants_on_vector()
+            places_past_the_end(0)
         act(T.x2[:], T.x1[:].indirect(T.nxl[:]), ["x1a", "x1b", "nxl"], ["x2"])
         walk(T.x1, ["x1a", "x1b"], T.ca, "ca", 0, 128)
         marks(64, 128, "xgb0")
-        diff(0, T.xg, "xga0", 0)
+        diff(0, T.xg, "xgv" if t and VM == 32 else "xga0", 0)
         diff(1, T.xg, "xga0", 0)
         wsum(T.p0, T.ca, "ca", 0, 128, "p0", "k1")
         walk(T.x1, ["x1a", "x1b"], T.ca, "ca", 128, 256)
@@ -323,43 +376,63 @@ def rank_program(g, core, T, topo):
         absc(3)
         wsum(T.p0, T.ca, "ca", 128, 256, "p0", "k1")
         act(T.x3[:], T.x2[:].indirect(T.nxl[:]), ["x2", "nxl"], ["x3"])
-        act(T.m1[:], T.p0[:, 0:256], ["k10", "k1128"], ["m1"], ["p0"])
+        act(T.rr[:, 0:256], T.p0[:, 0:256], ["k10", "k1128"], ["rr0"], ["p0"], func=F.Relu, bias=-8.0 * FAR)
+        if t == 0:
+            act(T.x4[:], T.x3[:].indirect(T.nxl[:]), ["x3", "nxl"], ["x4"])
         marks(128, 256, "xg1")
         walk(T.x2, ["x2"], T.cb, "cb", 0, 128)
         sums(T.p5, lambda k: T.ab[:, k:2048:16], ["ab0"], 0, 128, "p5", "sc0")
         wsum(T.p1, T.cb, "cb", 0, 128, "p1", "k2")
         walk(T.x2, ["x2"], T.cb, "cb", 128, 256)
+        wsum(T.p1, T.cb, "cb", 128, 256, "p1", "k2")
+        walk(T.x3, ["x3"], T.ca, "ca", 0, 128)
+        if t == 0:
+            wsum(T.p0, T.ca, "ca", 0, 128, "p0", "k3")
         diff(4, T.xg, "xg1", 0)
         diff(5, T.xg, "xg1", 0)
         absc(4)
         absc(5)
         diff(6, T.xg, "xg1", 0)
         diff(7, T.xg, "xg1", 0)
+        if t:
+            act(T.x4[:], T.x3[:].indirect(T.nxl[:]), ["x3", "nxl"], ["x4"])
         absc(6)
         absc(7)
-        wsum(T.p1, T.cb, "cb", 128, 256, "p1", "k2")
-        act(T.x4[:], T.x3[:].indirect(T.nxl[:]), ["x3", "nxl"], ["x4"])
-        walk(T.x3, ["x3"], T.ca, "ca", 0, 128)
-        sums(T.p5, lambda k: T.ab[:, 2048 + k::16], ["ab1"], 128, 256, "p5", "sc1")
-        wsum(T.p0, T.ca, "ca", 0, 128, "p0", "k3")
+        if t:
+            wsum(T.p0, T.ca, "ca", 0, 128, "p0", "k3")
         walk(T.x3, ["x3"], T.ca, "ca", 128, 256)
-        tt(T.m2[:], T.p1[:, 0:256], T.m1[:], A.max, ["k20", "k2128", "m1"], ["m2"], ["p1"])
+        act(T.rr[:, 256:512], T.p1[:, 0:256], ["k20", "k2128"], ["rr1"], ["p1"], func=F.Relu, bias=-8.0 * FAR)
+        if t == 0:
+            sums(T.p5, lambda k: T.ab[:, 2048 + k::16], ["ab1"], 128, 256, "p5", "sc1")
         wsum(T.p0, T.ca, "ca", 128, 256, "p0", "k3")
+        if t:
+            sums(T.p5, lambda k: T.ab[:, 2048 + k::16], ["ab1"], 128, 256, "p5", "sc1")
         act(T.xg4[:, 0:16 * LS], T.x4[:].indirect(T.d16[:, LV:256]), ["x4", "d16"], ["xg4"])
-        act(T.p6[:, 0:256], T.p5[:, 0:256], ["sc0", "sc1"], ["amb"], ["p5", "p6"], scale=32.0, bias=-131072.0)
-        act(T.p6[:, 256:512], T.p5[:, 0:256], ["sc0", "sc1", "c7"], ["bb"], ["p5", "p6"], scale=-16.0, bias=col(7))
         for c in range(LS // 32):
             pk = ("p2", "p3")[c % 2]
             diff(c, T.xg4, "xg4", LV)
-            act(T.sg4[:, 512 * c:512 * c + 512], T[pk][:], [pk + "d"], ["sg4"], [pk], func=F.Sign, bias=0.5)
+            act(T.sg4[:, 512 * c:512 * c + 512], T[pk][:], [pk + "d"], ["sg4"], [pk], func=F.Sign, scale=-1.0, bias=-0.5)
+            if c == 0:
+                act(T.m1[:], T.p5[:, 0:256], ["sc0", "sc1", "c9"], ["ka"], ["p5"], scale=16.0 / FAR, bias=col(9))
+                act(T.p6[:, 256:512], T.p5[:, 0:256], ["sc0", "sc1", "c7"], ["kb"], ["p5", "p6"], scale=-16.0 / FAR, bias=col(7))
         walk(T.x4, ["x4"], T.cb, "cb", 0, 128)
-        wsum(T.p1, T.cb, "cb", 0, 128, "p1", "k4")
+        act(T.rr[:, 512:768], T.p0[:, 0:256], ["k30", "k3128"], ["rr2"], ["p0"], func=F.Relu, bias=-8.0 * FAR)
+
+        def fourth(pout, p0, pk, w, wk, base, bk, src, sk, l0, l1, dk):
+            po = pout[:, p0 + l0:p0 + l1]
+            mm(po, base[:], T.ones[:, 0:l1 - l0], True, False, [bk, "ones"], [dk], [pk])
+            for j in range(2):
+                mm(po, w[:], T.rr[:, 256 * j + l0:256 * j + l1], False, False, [wk, "rr%d" % j], [dk], [pk])
+            for k in range(16):
+                mm(po, T.ek[:, 128 * k:128 * k + 128], src(k), False, False, ["ek", sk], [dk], [pk])
+            mm(po, w[:], T.rr[:, 512 + l0:512 + l1], False, True, [wk, "rr2"], [dk], [pk])
+
         walk(T.x4, ["x4"], T.cb, "cb", 128, LV)
-        sums(T.p5, lambda k: T.sg4[:, k:16 * LS:16], ["sg4"], LV, 256, "p5", "k4s")
-        wsum(T.p1, T.cb, "cb", 128, LV, "p1", "k4")
-        tt(T.m3[:], T.p0[:, 0:256], T.m2[:], A.max, ["k30", "k3128", "m2"], ["m3"], ["p0"])
-        ts(T.th[:, 0:LV], T.m3[:, 0:LV], 9.0, A.is_lt, ["m3"], ["th0"], (), 9.0, A.mult)
-        ts(T.th[:, LV:256], T.m3[:, LV:256], 9.0, A.is_ge, ["m3"], ["th1"], (), 17.0, A.mult)
+        fourth(T.p1, 0, "p1", T.i16, "i16", T.k8, "k8", lambda k: T.cb[:, k:2048:16], "cb0", 0, 128, "k40")
+        fourth(T.p5, 0, "p5", T.i32, "i32", T.kk1, "kk1", lambda k: T.sg4[:, k:16 * LS:16], "sg4", LV, 256, "k4s")
+        fourth(T.p0, 256, "p0", T.i16, "i16", T.k8, "k8", lambda k: T.cb[:, 2048 + k:16 * LV:16], "cb128", 128, LV, "k4128")
+        if t == 0:
+            later_constants()
         if t:
             act(T.vn[:], T.vl[:], ["vl"], ["vn"], scale=-1.0)
             act(T.vx[:], T.vl[:].indirect(T.exc[:]), ["vl", "exc"], ["vx"])
@@ -370,22 +443,22 @@ def rank_program(g, core, T, topo):
             for m, (o, n) in enumerate(SEG):
                 act(T.yv1[:, 256 + o:256 + o + n], T.vr[:, 256 - n:256], ["vr", "vn"], ["yv1"], func=F.Abs, bias=T.vn[:, m:m + 1])
             act(T.yv1[:, 0:256], T.p3[:, 0:256], ["dv"], ["yv1"], ["p3"], func=F.Abs)
-            act(T.ev[:], T.yv1[:], ["yv1"], ["ev"], func=F.Relu, scale=-1.0, bias=1.0)
-        tt(T.lt[:, LV:256], T.p5[:, LV:256], T.th[:, LV:256], A.is_ge, ["k4s", "th1"], ["lt1"], ["p5"])
-        tt(T.lt[:, 0:LV], T.p1[:, 0:LV], T.th[:, 0:LV], A.is_lt, ["k40", "k4128", "th0"], ["lt0"], ["p1"])
-        tt(T.tk[:], T.p6[:, 0:256], T.lt[:], A.mult, ["amb", "lt0", "lt1"], ["tk"], ["p6"])
-        tt(T.key[:], T.p6[:, 256:512], T.tk[:], A.add, ["bb", "tk"], ["key"], ["p6"])
-        vtr(T.keyt[:], T.key[:], ["key"], ["keyt"])
-        scan(T.s1[:], T.rst[:], T.keyt[:], A.max, A.min, ["rst", "keyt"], ["s1"])
-        tt(T.eqt[:], T.s1[:].indirect(T.exl[:]), T.keyt[:], A.is_equal, ["s1", "exl", "keyt"], ["eqt"])
-        tt(T.pd[:], T.p4[:, 0:256], T.eqt[:], A.mult, ["dt", "eqt"], ["pd"], ["p4"])
-        scan(T.s2[:], T.zr[:], T.pd[:], A.mult, A.add, ["zr", "pd"], ["s2"])
+        for h, parts in enumerate((((T.p1, "p1", 0, "k40", 0, 128),), ((T.p5, "p5", 0, "k4s", LV, 256), (T.p0, "p0", 256, "k4128", 128, LV)))):
+            H, k = slice(128 * h, 128 * h + 128), str(h)
+            for pp, pk, po, ck, l0, l1 in parts:
+                tt(T.tk[:, l0:l1], pp[:, po + l0:po + l1], T.m1[:, l0:l1], A.max, ["ka", ck], ["tk" + k], [pk])
+            tt(T.key[:, H], T.p6[:, 256 + 128 * h:384 + 128 * h], T.tk[:, H], A.min, ["tk" + k, "kb"], ["key" + k], ["p6"])
+            vtr(T.keyt[:, H], T.key[:, H], ["key" + k], ["keyt" + k])
+            scan(T.s1[:, H], T.rst[:, H], T.keyt[:, H], A.max, A.min, ["rst", "keyt" + k], ["s1" + k])
+            tt(T.eqt[:, H], T.s1[:, H].indirect(T.exl[:, 0:8]), T.keyt[:, H], A.is_equal, ["s1" + k, "exl", "keyt" + k], ["eqt" + k])
+            tt(T.pd[:, H], T.p4[:, H], T.eqt[:, H], A.mult, ["dt", "eqt" + k], ["pd" + k], ["p4"])
+            scan(T.s2[:, H], T.zr[:, H], T.pd[:, H], A.mult, A.add, ["zr", "pd" + k], ["s2" + k])
         for e in (0, 1):
             for h in (0, 1):
                 mm(T.p7[:, e:16:2], T.sw[:, 128 * (2 * e + h):128 * (2 * e + h) + 128], T.s2[:, 15 + 16 * h::32], h == 0, h == 1,
-                   ["sw", "s2"], ["a0"], ["p7"])
-        ts(T.fl[:], T.s1[:, 15::16], 0.0, A.is_ge, ["s1"], ["fl"])
-        vtr(T.oh[:], T.eqt[:], ["eqt"], ["oh"])
+                   ["sw", "s20", "s21"], ["a0"], ["p7"])
+        ts(T.fl[:], T.s1[:, 15::16], 0.0, A.is_ge, ["s10", "s11"], ["fl"])
+        vtr(T.oh[:], T.eqt[:], ["eqt0", "eqt1"], ["oh"])
         cp(T.a016[:], T.p7[:, 0:16], ["a0"], ["a016"], ["p7"])
         mm(T.p7[:, 32:48], T.ones[:], T.fl[:], True, True, ["ones", "fl"], ["nn"], ["p7"])
         sa, ra = T.sa[:, t:t + 1], T.ra[:, t:t + 1]
@@ -396,6 +469,10 @@ def rank_program(g, core, T, topo):
         act(col(19), col(18), ["n2"], ["n3"], bias=-MAG)
         act(sa, col(19), ["n3", "n4"], ["sa%d" % t], scale=-128.0, bias=col(20))
         send(t, "a", sa, "sa%d" % t, ra, "ra%d" % t)
+        if t == 0:
+            places_past_the_end(1)
+        if t:
+            act(T.ev[:], T.yv1[:], ["yv1"], ["ev"], func=F.Relu, scale=-1.0, bias=1.0)
         tt(T.w1[:], T.pvr[:].indirect(T.a016[:]), T.dg[:], A.mult, ["pvr", "a016", "dg"], ["w1"])
         scan(T.sc1[:], T.zr[:], T.w1[:], A.mult, A.add, ["zr", "w1"], ["sc1"])
         cp(T.bl[:, 0:16], T.sc1[:, 15::16], ["sc1"], ["bl0"])
@@ -411,12 +488,12 @@ def rank_program(g, core, T, topo):
         mm(T.p1[:, 256:512], T.idb[:], Q[:], True, False, ["idb", qk], ["xq"], ["p1"])
         mm(T.p6[:, 0:256], T.idfn[:], T.dd[:], True, False, ["idfn", "dd"], ["ad"], ["p6"])
         tt(T.d1[:], T.sc1[:, 15::16], T.p7[:, 0:16], A.subtract, ["sc1", "a0"], ["d1"], ["p7"])
-        ts(T.f1[:], T.p7[:, 16:32], 9.0, A.is_lt, ["b1"], ["f1"], ["p7"])
+        ts(T.f1[:], T.p7[:, 16:32], 9.0 * FAR, A.is_lt, ["b1"], ["f1"], ["p7"])
         tt(T.d2[:], T.sc2[:, 15::16], T.sc1[:, 15::16], A.subtract, ["sc1", "sc2"], ["d2"])
         tt(T.d1[:], T.d1[:], T.f1[:], A.mult, ["d1", "f1"], ["d1"])
         tt(T.d2[:], T.d2[:], T.f1[:], A.mult, ["d2", "f1"], ["d2"])
         tt(T.d1[:], T.d1[:], T.p7[:, 0:16], A.add, ["d1", "a0"], ["d1"], ["p7"])
-        ts(T.f2[:], T.p0[:, 0:16], 9.0, A.is_lt, ["b2"], ["f2"], ["p0"])
+        ts(T.f2[:], T.p0[:, 0:16], 9.0 * FAR, A.is_lt, ["b2"], ["f2"], ["p0"])
         tt(T.f2[:], T.f2[:], T.d2[:], A.mult, ["f2", "d2"], ["f2"])
         tt(T.al[:], T.f2[:], T.d1[:], A.add, ["f2", "d1"], ["al"])
         cp(T.al16[:], T.al[:], ["al"], ["al16"])
@@ -436,6 +513,9 @@ def rank_program(g, core, T, topo):
             cp(T.nl16[:], T.sc4[:, 15::16], ["sc4"], ["nl16"])
         cp(T.ar[:], T.ar32[:], ["ar32"], ["ar"])
         ts(T.we[:], T.sc3[:, 15::16], col(5), A.mult, ["sc3", "c5"], ["we"])
+        if t:
+            for m, (o, n) in enumerate([(-256, 256)] + SEG):
+                mm(T.p2[:, 256 - n:256], T.b4[:], T.ev[:, 256 + o:256 + o + n], m == 0, m == 15, ["b4", "ev"], ["cv_"], ["p2"])
         mm(T.p3[:, 0:256], T.idfn[:], T.ax[:], False, False, ["idfn", "ax"], ["da"], ["p3"])
         mm(T.p1[:, 256:512], T.idb[:], T.xga[:], False, True, ["idb", "xga"], ["xq"], ["p1"])
         mm(T.p3[:, 0:256], T.idh[:], T.ar[:], False, True, ["idh", "ar"], ["da"], ["p3"])
@@ -453,7 +533,8 @@ def rank_program(g, core, T, topo):
         if not last:
             act(T.qo[:], QN[:, 1::2], [qnk], ["qo"])
             send(t + 1, "q", T.qo[:], "qo", T["qr%d" % (t + 1)][:], "qr%d" % (t + 1))
-            for k in range(16):
+            repeat_q(range(16 - GK, 16), QN, qnk)
+            for k in range(16 - GK):
                 act(T.q16[:, k::16], T.y2[:], ["y2"], ["q16"], bias=-MAG)
         else:
             dma("y", "out", 64, [qnk], ["yq"], T.yq[:], QN[:])
@@ -463,24 +544,24 @@ def rank_program(g, core, T, topo):
         ts(T.ed[:], T.p3[:, 0:256], 0.0, A.is_equal, ["da"], ["ed"], ["p3"])
         mm(T.p5[:, 0:256], T.b4[:], T.ed[:], False, True, ["b4", "ed"], ["ca_"], ["p5"])
         tt(T.tk[:], T.p6[:, 0:256], T.oh[:], A.mult, ["ad", "oh"], ["ut"], ["p6"])
+        jobs = [("ca_", "p5", T.dgt, "dgt", T.al, "al", T.ap16, "ap16", (T.dm, T.ds, T.lx))]
         if t:
-            for m, (o, n) in enumerate([(-256, 256)] + SEG):
-                mm(T.p2[:, 256 - n:256], T.b4[:], T.ev[:, 256 + o:256 + o + n], m == 0, m == 15, ["b4", "ev"], ["cv_"], ["p2"])
-        place_of(T.p5[:, 0:256], "ca_", "p5", T.dgt, "dgt", T.al, "al", T.ap16, "ap16")
+            jobs = [("cv_", "p2", T.dgu, "dgu", T.vl, "vl", T.vp16, "vp16", (T.w1, T.sc1, T.d1))] + jobs
+        places(jobs)
         if not last:
             cp(T.nxr[:].indirect(T.ap16[:]), T.nx2[:], ["nx2", "ap16"], ["nxr"])
-            for b in range(8):
-                dma("y", "nd%d" % t, 128, ["nxr"], ["npf"], T.npf[:, 16 * b:16 * b + 16], T.nxr[16 * b:16 * b + 1, 0:2048])
+            dma("y", "nd%d" % t, 16, ["nxr"], ["npf"], T.npf[:], T.nxr[0:128:16, 0:2048])
         cp(T.xt[:].indirect(T.ap16[:]), T.xn[:], ["xn", "ap16"], ["xt"])
         if last:
             dma("y", "out", 64, ["xt"], ["yx"], T.yx[:], T.xt[:, 0:2048])
-        if t:
-            place_of(T.p2[:, 0:256], "cv_", "p2", T.dgu, "dgu", T.vl, "vl", T.vp16, "vp16")
         tt(T.vl[:], T.we[:], wrt[:], A.add, ["we", wk], ["vl"])
-        cp(T.vl16[:], T.vl[:], ["vl"], ["vl16"])
+        if last:
+            cp(T.vl16[:], T.vl[:], ["vl"], ["vl16"])
         tt(T.uw[:].indirect(T.vp16[:]), T.tk[:], T.dd[:], A.add, ["ut", "dd", "vp16"], ["uw"])
         if last:
             dma("y", "out", 64, ["uw"], ["yu"], T.yu[:], T.uw[:, 0:512])
+        else:
+            cp(T.vl16[:], T.vl[:], ["vl"], ["vl16"])
         Q, QN, qk, qnk = QN, Q, qnk, qk
     act(T.vr[:], T.idw[:].indirect(T.vl16[:]), ["idw", "vl16"], ["vr"])
     dma("y", "out", 64, ["vr"], ["yv"], T.yv[:], T.vr[0:128:16, :])

import numpy as np
from concourse.bass import DstId, RemoteDMATransfer
from concourse.mybir import dt, AluOpType as A, AxisListType, ActivationFunctionType as F

SCRATCH = {}
for _n, _c, _d in (
        ("xt", 2304, "bfloat16"), ("x1", 2048, "bfloat16"), ("x2", 2048, "bfloat16"), ("x3", 2048, "bfloat16"),
        ("x4", 2048, "bfloat16"), ("q16", 4096, "bfloat16"), ("qa", 256, "bfloat16"), ("qb", 256, "bfloat16"),
        ("qo", 128, "bfloat16"), ("qr0", 128, "bfloat16"), ("qr1", 128, "bfloat16"), ("qr2", 128, "bfloat16"),
        ("xg", 4096, "bfloat16"), ("ab", 4096, "bfloat16"), ("ca", 4096, "bfloat16"), ("cb", 4096, "bfloat16"),
        ("xg4", 2048, "bfloat16"), ("sg4", 2048, "bfloat16"),
        ("uw", 768, "float32"), ("ui", 512, "int32"), ("i16", 128, "bfloat16"), ("i32", 128, "bfloat16"), ("k8", 128, "bfloat16"), ("kk1", 128, "bfloat16"), ("nxr", 2304, "float32"),
        ("pvr", 2048, "int32"), ("rcr", 2048, "int32"), ("idw", 2048, "float32"),
        ("npi", 128, "int32"), ("npf", 128, "float32"), ("nxl", 128, "uint16"),
        ("dd", 256, "float32"), ("d16", 256, "uint16"), ("vl", 16, "float32"), ("vl16", 16, "uint16"),
        ("vn", 16, "float32"), ("vr", 256, "float32"), ("vx", 256, "float32"), ("yv1", 2176, "bfloat16"), ("ev", 2176, "bfloat16"),
        ("ar", 256, "float16"), ("ar32", 256, "float32"), ("ax", 256, "float32"), ("ed", 256, "bfloat16"),
        ("em", 1920, "bfloat16"), ("zz", 256, "bfloat16"),
        ("dm", 256, "float32"), ("ds", 256, "float32"), ("lx", 16, "float32"),
        ("vp16", 16, "uint16"), ("ap16", 16, "uint16"), ("m1", 256, "float32"), ("nph", 128, "float16"), ("npt", 128, "float16"),
        ("rr", 768, "bfloat16"), ("tk", 256, "float32"),
        ("key", 256, "float32"), ("keyt", 256, "float32"), ("s1", 256, "float32"), ("eqt", 256, "float32"),
        ("pd", 256, "float32"), ("s2", 256, "float16"), ("oh", 256, "float32"), ("fl", 16, "bfloat16"),
        ("a016", 16, "uint16"), ("w1", 256, "float32"), ("sc1", 256, "float32"), ("w2", 256, "float32"),
        ("sc2", 256, "float32"), ("bl", 32, "uint16"), ("xc", 512, "bfloat16"),
        ("f1", 16, "float32"), ("d1", 16, "float32"), ("d2", 16, "float32"), ("f2", 16, "float32"), ("al", 16, "float32"),
        ("al16", 16, "uint16"), ("w3", 256, "float32"), ("sc3", 256, "float32"), ("w4", 256, "float32"),
        ("sc4", 256, "float32"), ("ws", 16, "float32"), ("we", 16, "float32"), ("wr0", 16, "float32"),
        ("wr1", 16, "float32"), ("wr2", 16, "float32"), ("nl16", 16, "uint16"), ("nx2", 256, "float32"),
        ("xga", 256, "bfloat16"), ("h1", 256, "float32"), ("xn", 256, "bfloat16"),
        ("nj", 16, "float32"), ("cols", 64, "float32"), ("yy", 256, "float32"), ("y2", 256, "float32"),
        ("ci", 64, "int32"), ("cf", 256, "float32"), ("cg", 128, "float32"), ("ch", 128, "float32"),
        ("dg", 256, "float32"), ("dgt", 256, "float32"), ("dgu", 256, "float32"), ("tri", 256, "bfloat16"),
        ("rst", 256, "float32"), ("zr", 256, "float32"), ("ek", 2048, "bfloat16"), ("cc", 128, "bfloat16"),
        ("b4", 128, "bfloat16"), ("idf", 128, "float32"), ("idfn", 128, "float32"), ("idb", 128, "bfloat16"),
        ("idn", 128, "bfloat16"), ("idh", 128, "float16"), ("sw", 512, "float16"), ("ones", 128, "bfloat16"),
        ("exl", 16, "uint16"), ("exc", 16, "uint16"), ("sa", 4, "float32"), ("ra", 4, "float32")):
    _d = {"w1": "float16", "w2": "float16", "w3": "float16", "w4": "float16", "sc1": "float16", "sc2": "float16",
          "sc3": "float16", "sc4": "float16", "dm": "float16", "ds": "float16", "pd": "float16",
          "zr": "bfloat16", "eqt": "bfloat16", "oh": "bfloat16"}.get(_n, _d)
    SCRATCH[_n] = ("sbuf", [128, 2560 if _c == 2304 else _c], _d)
for _k in range(8):
    SCRATCH["p%d" % _k] = ("psum", [128, 512], "float32")

SCRATCH["nxd"] = ("dram", [8, 2048], "float32")

ROUNDS = 3
LSS = (64, 64, 64)
XV0, XV = 512, 1024
SEMAPHORES = ["cv", "cs", "ct", "cp", "ldx", "ldq", "ldu", "ldn", "ldr", "ldd", "ldp", "ldc", "nd0", "nd1", "out"]
for _t in range(ROUNDS):
    SEMAPHORES += ["%s%d" % (_a, _t) for _a in ("rq", "ra", "rw", "lq", "la", "lw")]
GK0, GK = 4, 8
VM = 0
FAR = 262144.0
BIG = 1048576.0
MAG = 12582912.0


def rank_program(g, core, T, topo):
    rank = T.rank_of(core)
    if rank is None:
        return
    N = len(T.cores)
    V, S, P = g.vector, g.scalar, g.tensor
    eng = {"v": V, "s": S, "t": P, "p": g, "y": g.sync}
    own = {"v": "cv", "s": "cs", "t": "ct", "p": "cp"}
    total = {}
    known = {e: {} for e in eng}
    clocks = {}
    wr, rd, bank = {}, {}, {}

    def need(e, deps):
        for s in sorted(deps):
            n = deps[s]
            if known[e].get(s, 0) >= n:
                continue
            eng[e].wait_ge(T.sem[s], n)
            for k, c in clocks.get((s, n), {}).items():
                known[e][k] = max(known[e].get(k, 0), c)
            known[e][s] = n

    def deps_of(R, W, X, me):
        d = {}

        def put(s, n):
            d[s] = max(d.get(s, 0), n)
        for k in R:
            if k in wr:
                put(*wr[k])
        for k in W:
            if k in wr and wr[k][0] != me:
                put(*wr[k])
            for s, n in rd.get(k, {}).items():
                if s != me:
                    put(s, n)
        for k in X:
            for s, n in bank.get(k, {}).items():
                if s != me:
                    put(s, n)
        return d

    def note(s, n, R, W, X):
        for k in R:
            rd.setdefault(k, {})[s] = n
        for k in W:
            wr[k] = (s, n)
            rd[k] = {}
        for k in X:
            bank.setdefault(k, {})[s] = n

    def op(e, R, W, X, call):
        me = own[e]
        need(e, deps_of(R, W, X, me))
        n = total.get(me, 0) + 1
        total[me] = n
        call().then_inc(T.sem[me], 1)
        c = dict(known[e])
        c[me] = n
        clocks[(me, n)] = c
        note(me, n, R, W, X)

    def dma(e, sem, full, R, W, out, in_):
        need(e, deps_of(R, W, [], sem))
        total[sem] = total.get(sem, 0) + 16
        eng[e].dma_start(out, in_).then_inc(T.sem[sem], 16)
        c = dict(known[e])
        c[sem] = full
        clocks[(sem, full)] = c
        note(sem, full, R, W, [])

    def send(t, kind, src, key, dst, land):
        d = T.cores[(rank + 1 + t % (N - 1)) % N]
        es = topo.engines(core, d)[:8]
        m = 0
        for x in es:
            m |= 1 << x
        need("p", deps_of([key], [], [], None))
        rid, pid = topo.addr(d, core)
        rs, ls = "r" + kind + str(t), "l" + kind + str(t)
        g.remote_dma(dst, src, T.sem[rs], T.sem[ls], pid, rid, m)
        total[ls] = len(es)
        note(ls, len(es), [key], [], [])
        sender = T.cores[(rank - 1 - t % (N - 1)) % N]
        total[rs] = len(topo.engines(sender, core)[:8])
        wr[land] = (rs, total[rs])

    def act(out, in_, R, W, X=(), func=F.Identity, **kw):
        op("s", R, W, X, lambda: S.activation(out, in_, func, **kw))

    def tt(out, a, b, o, R, W, X=()):
        op("v", R, W, X, lambda: V.tensor_tensor(out, a, b, o))

    def ts(out, a, s1, o1, R, W, X=(), s2=None, o2=None):
        if o2 is None:
            op("v", R, W, X, lambda: V.tensor_scalar(out, a, s1, None, o1))
        else:
            op("v", R, W, X, lambda: V.tensor_scalar(out, a, s1, s2, o1, o2))

    def cp(out, in_, R, W, X=()):
        op("v", R, W, X, lambda: V.tensor_copy(out, in_))

    def vtr(out, in_, R, W, X=()):
        op("v", R, W, X, lambda: V.transpose(out, in_))

    def scan(out, d0, d1, o0, o1, R, W):
        op("v", R, W, [], lambda: V.tensor_tensor_scan(out, d0, d1, 0.0, o0, o1))

    def mm(out, l, r, st, sp, R, W, X):
        op("t", R, W, X, lambda: P.matmul(out, l, r, st, sp))

    def iota(out, pat, base, cm, W, whole=False):
        if whole:
            op("p", [], W, [], lambda: g.iota(out, pat, base, cm))
        else:
            op("p", [], W, [], lambda: g.iota(out, pat, base, cm, allow_small_or_imprecise_dtypes=True))

    def col(j):
        return T.cols[:, j:j + 1]

    dma("y", "ldn", 16, [], ["npi"], T.npi[:], T.nx[:])
    dma("y", "ldx", 16, [], ["xt"], T.xt[:, 0:2048], T.xd[:])
    dma("s", "ldq", 16, [], ["qa"], T.qa[:], T.mv[:])
    dma("s", "ldu", 16, [], ["ui"], T.ui[:], T.ul[:])
    for s, dst, src, k in (("ldp", T.pvr, T.pv, "pvr"), ("ldc", T.rcr, T.rc, "rcr")):
        for i in range(16):
            dma("y", s, 256, ["xt", "ui", "qa"], [k], dst[i:128:16, :], src[:])

    def repeat_nx():
        dma("y", "ldd", 16, ["npf"], ["nxd"], T.nxd[:], T.npf[:])
        for i in range(16):
            dma("y", "ldr", 256, ["nxd"], ["nxr"], T.nxr[i:128:16, 0:2048], T.nxd[:])

    iota(T.ch[:], [[1, 128]], 0, -1, ["ch"])
    iota(T.ci[:, 0:1], [[0, 1]], 0, 1, ["ci0"], True)
    iota(T.cf[:], [[0, 16], [1, 16]], 0, 0, ["cf"])
    iota(T.cg[:], [[1, 8], [0, 16]], 0, 0, ["cg"])
    ts(T.idf[:], T.ch[:], 0.0, A.is_equal, ["ch"], ["idf"])
    op("v", ["ci0"], ["ci3"], [], lambda: V.tensor_scalar(T.ci[:, 1:2], T.ci[:, 0:1], 15, None, A.bitwise_and))
    op("v", ["ci0"], ["ci4"], [], lambda: V.tensor_scalar(T.ci[:, 2:3], T.ci[:, 0:1], 4, None, A.arith_shift_right))
    op("v", ["ci0"], ["ci6"], [], lambda: V.tensor_scalar(T.ci[:, 4:5], T.ci[:, 0:1], 1, None, A.bitwise_and))
    cp(col(0), T.ci[:, 1:2], ["ci3"], ["c0"])
    cp(col(1), T.ci[:, 2:3], ["ci4"], ["c1"])
    op("v", ["ci4"], ["ci5"], [], lambda: V.tensor_scalar(T.ci[:, 3:4], T.ci[:, 2:3], 1, None, A.bitwise_and))
    cp(col(4), T.ci[:, 4:5], ["ci6"], ["c4"])
    ts(T.idb[:], T.ch[:], 0.0, A.is_equal, ["ch"], ["idb"])
    cp(col(2), T.ci[:, 3:4], ["ci5"], ["c2"])
    ts(col(3), T.ci[:, 3:4], 0.0, A.is_equal, ["ci5"], ["c3"])
    ts(T.idn[:], T.ch[:], 0.0, A.is_equal, ["ch"], ["idn"], (), -1.0, A.mult)
    ts(T.m1[:, 0:128], T.cg[:], col(1), A.is_equal, ["cg", "c1"], ["bs"])
    ts(T.m1[:, 128:256], T.cf[:, 0:128], 1.0, A.add, ["cf"], ["cg2"])
    tt(T.cc[:], T.m1[:, 0:128], T.m1[:, 128:256], A.mult, ["bs", "cg2"], ["cc"])
    act(T.zr[:], T.cf[:], ["cf"], ["zr"], func=F.Sign)
    act(T.rst[:], T.zr[:], ["zr"], ["rst"], scale=-2.0 * BIG, bias=BIG)
    act(col(8), col(0), ["c0"], ["c8"], bias=0.5)
    act(T.y2[:], T.cf[:], ["cf", "c8"], ["tri0"], scale=-1.0, bias=col(8), func=F.Sign)
    act(T.tri[:], T.y2[:], ["tri0"], ["tri"], scale=4096.0, func=F.Relu)
    act(T.qo[:], T.qa[:, 1::2], ["qa"], ["qo"])
    send(0, "q", T.qo[:], "qo", T.qr0[:], "qr0")

    def repeat_q(ks, q, qk):
        for k in ks:
            op("p", [qk], ["q16g"], [], lambda: g.affine_select(T.q16[:, k::16], q[:], [[0, 256]], A.is_gt, 0.0, 1, 0))

    repeat_q(range(16 - GK0, 16), T.qa, "qa")
    iota(T.ci[:, 16:32], [[16, 16]], 15, 0, ["ci1"], True)
    iota(T.ci[:, 32:48], [[1, 16]], 0, 0, ["ci2"], True)
    iota(T.nj[:], [[32, 16]], 0, 0, ["nj"])
    iota(T.dgt[:], [[2, 256]], 2048, 0, ["dgt0"])
    iota(T.dgu[:], [[1, 256]], 512, 0, ["dgu0"])
    iota(T.idw[:], [[1, 2048]], 0, 0, ["idw"])

    def make_ek(ks):
        for k in ks:
            ts(T.ek[:, 128 * k:128 * k + 128], T.cc[:], float(k + 1), A.is_equal, ["cc"], ["ek"], (), FAR, A.mult)

    make_ek(range(8))
    cp(T.d16[:], T.ui[:, 0:512:2], ["ui"], ["d16"])
    cp(T.nph[:], T.npi[:], ["npi"], ["nph"])
    cp(T.npf[:], T.npi[:], ["npi"], ["npf"])
    repeat_nx()

    def list_of_nx():
        vtr(T.npt[:], T.nph[:], ["nph"], ["npt"])
        for e in (0, 1):
            for b in range(4):
                for h in (0, 1):
                    mm(T.p7[:, 2 * b + e:128:8], T.sw[:, 128 * (2 * e + h):128 * (2 * e + h) + 128],
                       T.npt[:, 32 * b + 16 * h:32 * b + 16 * h + 16], h == 0, h == 1, ["sw", "npt"], ["nxt"], ["p7"])

    for j, (x, c) in enumerate(((0.0, 3), (16.0, 3), (-16.0, 2), (0.0, 2))):
        ts(T.sw[:, 128 * j:128 * j + 128], T.ch[:], x, A.is_equal, ["ch", "c%d" % c], ["sw"], (), col(c), A.mult)
    list_of_nx()
    make_ek(range(8, 16))
    cp(T.nxl[:], T.p7[:, 0:128], ["nxt"], ["nxl"], ["p7"])
    cp(T.dd[:], T.ui[:, 0:512:2], ["ui"], ["dd"])

    def first_fill():
        for k in range(16 - GK0):
            cp(T.q16[:, k::16], T.qa[:], ["qa"], ["q16"])
        vtr(T.p4[:, 0:256], T.dd[:], ["dd"], ["dt"], ["p4"])

    def constants_on_scalar():
        act(col(5), col(4), ["c4"], ["c5"], scale=-1.0, bias=1.0)
        act(col(6), col(0), ["c0"], ["c6"], scale=2.0)
        act(col(7), col(0), ["c0"], ["c7"], bias=65536.0)
        act(col(9), col(0), ["c0"], ["c9"], bias=-65536.0)
        for w, k, x in ((T.i16, "i16", 16.0), (T.i32, "i32", 32.0), (T.k8, "k8", -8.4 * FAR), (T.kk1, "kk1", -FAR)):
            act(w[:], T.idb[:], ["idb"], [k], scale=x)
        act(T.idfn[:], T.idf[:], ["idf"], ["idfn"], scale=-1.0)
        act(T.ones[:], T.cf[:, 0:128], ["cf"], ["ones"], scale=0.0, bias=1.0)
        act(T.zz[:], T.cf[:], ["cf"], ["zz"], scale=0.0)

    def constants_on_vector():
        ts(T.dg[:], T.cf[:], col(0), A.is_equal, ["cf", "c0"], ["dg"])

    def later_constants():
        ts(T.b4[:], T.cc[:], 0.0, A.is_gt, ["cc"], ["b4"], (), 4096.0, A.mult)
        ts(T.idh[:], T.ch[:], 0.0, A.is_equal, ["ch"], ["idh"])
        cp(T.exl[:], T.ci[:, 16:32], ["ci1"], ["exl"])
        cp(T.exc[:], T.ci[:, 32:48], ["ci2"], ["exc"])
        ts(T.vl[:], T.nj[:], col(6), A.add, ["nj", "c6"], ["vl"])
        cp(T.vp16[:], T.vl[:], ["vl"], ["vp16"])
        cp(T.uw[:, 0:512], T.ui[:], ["ui"], ["uw"])

    def places_past_the_end(step):
        if step == 0:
            act(T.yy[:], T.dg[:], ["dg"], ["dgs"], scale=4096.0, bias=-4096.0)
        for w, k, pb in ((T.dgt, "dgt", "p4"), (T.dgu, "dgu", "p5")):
            pw = T[pb][:, 256:512]
            if step == 0:
                mm(pw, T.idf[:], w[:], True, False, ["idf", k + "0"], [k + "p"], [pb])
                mm(pw, T.idf[:], T.yy[:], False, True, ["idf", "dgs"], [k + "p"], [pb])
            else:
                act(w[:], pw, [k + "p"], [k], [pb], func=F.Relu)

    def places(jobs):
        for cb, pk, dgx, dk, al, alk, out16, outk, (dm, ds, lx) in jobs:
            tt(dm[:], T[pk][:, 0:256], dgx[:], A.min, [cb, dk], ["dm" + pk], [pk])
        for cb, pk, dgx, dk, al, alk, out16, outk, (dm, ds, lx) in jobs:
            scan(ds[:], T.zr[:], dm[:], A.mult, A.add, ["zr", "dm" + pk], ["ds" + pk])
        for cb, pk, dgx, dk, al, alk, out16, outk, (dm, ds, lx) in jobs:
            tt(lx[:], ds[:, 15::16], al[:], A.max, ["ds" + pk, alk], ["lx" + pk])
        for cb, pk, dgx, dk, al, alk, out16, outk, (dm, ds, lx) in jobs:
            cp(out16[:], lx[:], ["lx" + pk], [outk])

    def sums(pout, src, keys, l0, l1, pk, dk):
        for k in range(16):
            mm(pout[:, l0:l1], T.ek[:, 128 * k:128 * k + 128], src(k), k == 0, k == 15, ["ek"] + keys, [dk], [pk])

    SEG = [(0, 0)] * 15
    _o = 0
    for m in range(15):
        SEG[m] = (_o, 240 - 16 * m)
        _o += 240 - 16 * m

    Q, QN, qk, qnk = T.qa, T.qb, "qa", "qb"
    for t in range(ROUNDS):
        last = t == ROUNDS - 1
        LS = LSS[t]
        LV = 256 - LS
        xv = XV if t else XV0

        def walk(x, xk, out, ok, l0, l1):
            tt(out[:, 16 * l0:16 * l1], x[:].indirect(T.d16[:, l0:l1]), T.q16[:, 16 * l0:16 * l1], A.is_lt,
               xk + ["d16", "q16", "q16g"], [ok + str(l0)])

        def wsum(pout, out, ok, l0, l1, pk, dk):
            sums(pout, lambda k: out[:, 16 * l0 + k:16 * l1:16], [ok + str(l0)], l0, l1, pk, dk + str(l0))

        def diff(c, src, sk, lane0):
            pk = ("p2", "p3")[c % 2]
            j = 512 * c
            mm(T[pk][:], T.idb[:], src[:, j:j + 512], True, False, ["idb", sk], [pk + "d"], [pk])
            mm(T[pk][:], T.idn[:], T.q16[:, 16 * lane0 + j:16 * lane0 + j + 512], False, True, ["idn", "q16", "q16g"], [pk + "d"], [pk])

        def absc(c):
            pk = ("p2", "p3")[c % 2]
            act(T.ab[:, 512 * c:512 * c + 512], T[pk][:], [pk + "d"], ["ab%d" % (c // 4)], [pk], func=F.Abs)

        def marks(l0, l1, k):
            act(T.xg[:, 16 * l0:16 * l1], T.xt[:, 0:2048].indirect(T.d16[:, l0:l1]), ["xt", "d16"], [k])

        if t:
            cp(T.d16[:], T.uw[:, 0:512].indirect(T.vl16[:]), ["uw", "vl16"], ["d16"])
            act(T.dd[:], T.uw[:, 0:512].indirect(T.vl16[:]), ["uw", "vl16"], ["dd"])
            marks(VM, 64, "xga0")
            vtr(T.p4[:, 0:256], T.dd[:], ["dd"], ["dt"], ["p4"])
            if VM:
                cp(T.xg[:, 0:16 * VM], T.xt[:, 0:2048].indirect(T.d16[:, 0:VM]), ["xt", "d16"], ["xgv"])
            cp(T.nph[:], T.npf[:], ["npf"], ["nph"])
            list_of_nx()
            cp(T.nxl[:], T.p7[:, 0:128], ["nxt"], ["nxl"], ["p7"])
            cp(T.x1[:, 0:xv], T.xt[:, 0:2048].indirect(T.nxl[:, 0:xv // 16]), ["xt", "nxl"], ["x1a"])
        else:
            constants_on_scalar()
        act(T.x1[:, xv:2048], T.xt[:, 0:2048].indirect(T.nxl[:, xv // 16:128]), ["xt", "nxl"], ["x1b"])
        if t == 0:
            marks(0, 64, "xga0")
            first_fill()
            cp(T.x1[:, 0:xv], T.xt[:, 0:2048].indirect(T.nxl[:, 0:xv // 16]), ["xt", "nxl"], ["x1a"])
            constants_on_vector()
            places_past_the_end(0)
        act(T.x2[:], T.x1[:].indirect(T.nxl[:]), ["x1a", "x1b", "nxl"], ["x2"])
        walk(T.x1, ["x1a", "x1b"], T.ca, "ca", 0, 128)
        marks(64, 128, "xgb0")
        diff(0, T.xg, "xgv" if t and VM == 32 else "xga0", 0)
        diff(1, T.xg, "xga0", 0)
        wsum(T.p0, T.ca, "ca", 0, 128, "p0", "k1")
        walk(T.x1, ["x1a", "x1b"], T.ca, "ca", 128, 256)
        absc(0)
        absc(1)
        diff(2, T.xg, "xgb0", 0)
        diff(3, T.xg, "xgb0", 0)
        absc(2)
        absc(3)
        wsum(T.p0, T.ca, "ca", 128, 256, "p0", "k1")
        act(T.x3[:], T.x2[:].indirect(T.nxl[:]), ["x2", "nxl"], ["x3"])
        act(T.rr[:, 0:256], T.p0[:, 0:256], ["k10", "k1128"], ["rr0"], ["p0"], func=F.Relu, bias=-8.0 * FAR)
        if t == 0:
            act(T.x4[:], T.x3[:].indirect(T.nxl[:]), ["x3", "nxl"], ["x4"])
        marks(128, 256, "xg1")
        walk(T.x2, ["x2"], T.cb, "cb", 0, 128)
        sums(T.p5, lambda k: T.ab[:, k:2048:16], ["ab0"], 0, 128, "p5", "sc0")
        wsum(T.p1, T.cb, "cb", 0, 128, "p1", "k2")
        walk(T.x2, ["x2"], T.cb, "cb", 128, 256)
        wsum(T.p1, T.cb, "cb", 128, 256, "p1", "k2")
        walk(T.x3, ["x3"], T.ca, "ca", 0, 128)
        if t == 0:
            wsum(T.p0, T.ca, "ca", 0, 128, "p0", "k3")
        diff(4, T.xg, "xg1", 0)
        diff(5, T.xg, "xg1", 0)
        absc(4)
        absc(5)
        diff(6, T.xg, "xg1", 0)
        diff(7, T.xg, "xg1", 0)
        if t:
            act(T.x4[:], T.x3[:].indirect(T.nxl[:]), ["x3", "nxl"], ["x4"])
        absc(6)
        absc(7)
        if t:
            wsum(T.p0, T.ca, "ca", 0, 128, "p0", "k3")
        walk(T.x3, ["x3"], T.ca, "ca", 128, 256)
        act(T.rr[:, 256:512], T.p1[:, 0:256], ["k20", "k2128"], ["rr1"], ["p1"], func=F.Relu, bias=-8.0 * FAR)
        if t == 0:
            sums(T.p5, lambda k: T.ab[:, 2048 + k::16], ["ab1"], 128, 256, "p5", "sc1")
        wsum(T.p0, T.ca, "ca", 128, 256, "p0", "k3")
        if t:
            sums(T.p5, lambda k: T.ab[:, 2048 + k::16], ["ab1"], 128, 256, "p5", "sc1")
        act(T.xg4[:, 0:16 * LS], T.x4[:].indirect(T.d16[:, LV:256]), ["x4", "d16"], ["xg4"])
        for c in range(LS // 32):
            pk = ("p2", "p3")[c % 2]
            diff(c, T.xg4, "xg4", LV)
            act(T.sg4[:, 512 * c:512 * c + 512], T[pk][:], [pk + "d"], ["sg4"], [pk], func=F.Sign, scale=-1.0, bias=-0.5)
            if c == 0:
                act(T.m1[:], T.p5[:, 0:256], ["sc0", "sc1", "c9"], ["ka"], ["p5"], scale=16.0 / FAR, bias=col(9))
                act(T.p6[:, 256:512], T.p5[:, 0:256], ["sc0", "sc1", "c7"], ["kb"], ["p5", "p6"], scale=-16.0 / FAR, bias=col(7))
        walk(T.x4, ["x4"], T.cb, "cb", 0, 128)
        act(T.rr[:, 512:768], T.p0[:, 0:256], ["k30", "k3128"], ["rr2"], ["p0"], func=F.Relu, bias=-8.0 * FAR)

        def fourth(pout, p0, pk, w, wk, base, bk, src, sk, l0, l1, dk):
            po = pout[:, p0 + l0:p0 + l1]
            mm(po, base[:], T.ones[:, 0:l1 - l0], True, False, [bk, "ones"], [dk], [pk])
            for j in range(2):
                mm(po, w[:], T.rr[:, 256 * j + l0:256 * j + l1], False, False, [wk, "rr%d" % j], [dk], [pk])
            for k in range(16):
                mm(po, T.ek[:, 128 * k:128 * k + 128], src(k), False, False, ["ek", sk], [dk], [pk])
            mm(po, w[:], T.rr[:, 512 + l0:512 + l1], False, True, [wk, "rr2"], [dk], [pk])

        walk(T.x4, ["x4"], T.cb, "cb", 128, LV)
        fourth(T.p1, 0, "p1", T.i16, "i16", T.k8, "k8", lambda k: T.cb[:, k:2048:16], "cb0", 0, 128, "k40")
        fourth(T.p5, 0, "p5", T.i32, "i32", T.kk1, "kk1", lambda k: T.sg4[:, k:16 * LS:16], "sg4", LV, 256, "k4s")
        fourth(T.p0, 256, "p0", T.i16, "i16", T.k8, "k8", lambda k: T.cb[:, 2048 + k:16 * LV:16], "cb128", 128, LV, "k4128")
        if t == 0:
            later_constants()
        if t:
            act(T.vn[:], T.vl[:], ["vl"], ["vn"], scale=-1.0)
            act(T.vx[:], T.vl[:].indirect(T.exc[:]), ["vl", "exc"], ["vx"])
            act(T.vr[:], T.idw[:].indirect(T.vl16[:]), ["idw", "vl16"], ["vr"])
            mm(T.p3[:, 0:256], T.idfn[:], T.vx[:], True, False, ["idfn", "vx"], ["dv"], ["p3"])
            mm(T.p3[:, 0:256], T.idf[:], T.vr[:], False, False, ["idf", "vr"], ["dv"], ["p3"])
            mm(T.p3[:, 0:256], T.idb[:], T.tri[:], False, True, ["idb", "tri"], ["dv"], ["p3"])
            for m, (o, n) in enumerate(SEG):
                act(T.yv1[:, 256 + o:256 + o + n], T.vr[:, 256 - n:256], ["vr", "vn"], ["yv1"], func=F.Abs, bias=T.vn[:, m:m + 1])
            act(T.yv1[:, 0:256], T.p3[:, 0:256], ["dv"], ["yv1"], ["p3"], func=F.Abs)
        for h, parts in enumerate((((T.p1, "p1", 0, "k40", 0, 128),), ((T.p5, "p5", 0, "k4s", LV, 256), (T.p0, "p0", 256, "k4128", 128, LV)))):
            H, k = slice(128 * h, 128 * h + 128), str(h)
            for pp, pk, po, ck, l0, l1 in parts:
                tt(T.tk[:, l0:l1], pp[:, po + l0:po + l1], T.m1[:, l0:l1], A.max, ["ka", ck], ["tk" + k], [pk])
            tt(T.key[:, H], T.p6[:, 256 + 128 * h:384 + 128 * h], T.tk[:, H], A.min, ["tk" + k, "kb"], ["key" + k], ["p6"])
            vtr(T.keyt[:, H], T.key[:, H], ["key" + k], ["keyt" + k])
            scan(T.s1[:, H], T.rst[:, H], T.keyt[:, H], A.max, A.min, ["rst", "keyt" + k], ["s1" + k])
            tt(T.eqt[:, H], T.s1[:, H].indirect(T.exl[:, 0:8]), T.keyt[:, H], A.is_equal, ["s1" + k, "exl", "keyt" + k], ["eqt" + k])
            tt(T.pd[:, H], T.p4[:, H], T.eqt[:, H], A.mult, ["dt", "eqt" + k], ["pd" + k], ["p4"])
            scan(T.s2[:, H], T.zr[:, H], T.pd[:, H], A.mult, A.add, ["zr", "pd" + k], ["s2" + k])
        for e in (0, 1):
            for h in (0, 1):
                mm(T.p7[:, e:16:2], T.sw[:, 128 * (2 * e + h):128 * (2 * e + h) + 128], T.s2[:, 15 + 16 * h::32], h == 0, h == 1,
                   ["sw", "s20", "s21"], ["a0"], ["p7"])
        ts(T.fl[:], T.s1[:, 15::16], 0.0, A.is_ge, ["s10", "s11"], ["fl"])
        vtr(T.oh[:], T.eqt[:], ["eqt0", "eqt1"], ["oh"])
        cp(T.a016[:], T.p7[:, 0:16], ["a0"], ["a016"], ["p7"])
        mm(T.p7[:, 32:48], T.ones[:], T.fl[:], True, True, ["ones", "fl"], ["nn"], ["p7"])
        sa, ra = T.sa[:, t:t + 1], T.ra[:, t:t + 1]
        act(T.nj[:], T.p7[:, 32:48], ["nn"], ["nj", "n"], ["p7"], accum_out=col(16))
        act(col(17), col(16), ["n"], ["n1"], scale=1.0 / 256, bias=-0.498046875)
        act(col(20), col(16), ["n"], ["n4"], scale=0.5, bias=-0.25)
        act(col(18), col(17), ["n1"], ["n2"], bias=MAG)
        act(col(19), col(18), ["n2"], ["n3"], bias=-MAG)
        act(sa, col(19), ["n3", "n4"], ["sa%d" % t], scale=-128.0, bias=col(20))
        send(t, "a", sa, "sa%d" % t, ra, "ra%d" % t)
        if t == 0:
            places_past_the_end(1)
        if t:
            act(T.ev[:], T.yv1[:], ["yv1"], ["ev"], func=F.Relu, scale=-1.0, bias=1.0)
        tt(T.w1[:], T.pvr[:].indirect(T.a016[:]), T.dg[:], A.mult, ["pvr", "a016", "dg"], ["w1"])
        scan(T.sc1[:], T.zr[:], T.w1[:], A.mult, A.add, ["zr", "w1"], ["sc1"])
        cp(T.bl[:, 0:16], T.sc1[:, 15::16], ["sc1"], ["bl0"])
        tt(T.w2[:], T.pvr[:].indirect(T.bl[:, 0:16]), T.dg[:], A.mult, ["pvr", "bl0", "dg"], ["w2"])
        tt(T.xc[:, 0:256], T.xt[:, 0:2048].indirect(T.bl[:, 0:16]), Q[:], A.is_lt, ["xt", "bl0", qk], ["xc0"])
        sums(T.p7, lambda k: T.xc[:, k:256:16], ["xc0"], 16, 32, "p7", "b1")
        scan(T.sc2[:], T.zr[:], T.w2[:], A.mult, A.add, ["zr", "w2"], ["sc2"])
        cp(T.bl[:, 16:32], T.sc2[:, 15::16], ["sc2"], ["bl1"])
        tt(T.xc[:, 256:512], T.xt[:, 0:2048].indirect(T.bl[:, 16:32]), Q[:], A.is_lt, ["xt", "bl1", qk], ["xc1"])
        sums(T.p0, lambda k: T.xc[:, 256 + k::16], ["xc1"], 0, 16, "p0", "b2")
        mm(T.p5[:, 0:256], T.b4[:], T.zz[:], True, False, ["b4", "zz"], ["ca_"], ["p5"])
        mm(T.p3[:, 0:256], T.idb[:], T.tri[:], True, False, ["idb", "tri"], ["da"], ["p3"])
        mm(T.p1[:, 256:512], T.idb[:], Q[:], True, False, ["idb", qk], ["xq"], ["p1"])
        mm(T.p6[:, 0:256], T.idfn[:], T.dd[:], True, False, ["idfn", "dd"], ["ad"], ["p6"])
        tt(T.d1[:], T.sc1[:, 15::16], T.p7[:, 0:16], A.subtract, ["sc1", "a0"], ["d1"], ["p7"])
        ts(T.f1[:], T.p7[:, 16:32], 9.0 * FAR, A.is_lt, ["b1"], ["f1"], ["p7"])
        tt(T.d2[:], T.sc2[:, 15::16], T.sc1[:, 15::16], A.subtract, ["sc1", "sc2"], ["d2"])
        tt(T.d1[:], T.d1[:], T.f1[:], A.mult, ["d1", "f1"], ["d1"])
        tt(T.d2[:], T.d2[:], T.f1[:], A.mult, ["d2", "f1"], ["d2"])
        tt(T.d1[:], T.d1[:], T.p7[:, 0:16], A.add, ["d1", "a0"], ["d1"], ["p7"])
        ts(T.f2[:], T.p0[:, 0:16], 9.0 * FAR, A.is_lt, ["b2"], ["f2"], ["p0"])
        tt(T.f2[:], T.f2[:], T.d2[:], A.mult, ["f2", "d2"], ["f2"])
        tt(T.al[:], T.f2[:], T.d1[:], A.add, ["f2", "d1"], ["al"])
        cp(T.al16[:], T.al[:], ["al"], ["al16"])
        tt(T.w3[:], T.rcr[:].indirect(T.al16[:]), T.dg[:], A.mult, ["rcr", "al16", "dg"], ["w3"])
        act(T.ar32[:], T.idw[:].indirect(T.al16[:]), ["idw", "al16"], ["ar32"])
        act(T.ax[:], T.al[:].indirect(T.exc[:]), ["al", "exc"], ["ax"])
        act(T.xga[:], T.xt[:, 0:2048].indirect(T.al16[:]), ["xt", "al16"], ["xga"])
        if not last:
            tt(T.w4[:], T.nxr[:, 0:2048].indirect(T.al16[:]), T.dg[:], A.mult, ["nxr", "al16", "dg"], ["w4"])
        scan(T.sc3[:], T.zr[:], T.w3[:], A.mult, A.add, ["zr", "w3"], ["sc3"])
        if not last:
            scan(T.sc4[:], T.zr[:], T.w4[:], A.mult, A.add, ["zr", "w4"], ["sc4"])
        ts(T.ws[:], T.sc3[:, 15::16], col(4), A.mult, ["sc3", "c4"], ["ws"])
        wrt, wk = T["wr%d" % t], "wr%d" % t
        send(t, "w", T.ws[:], "ws", wrt[:], wk)
        if not last:
            cp(T.nl16[:], T.sc4[:, 15::16], ["sc4"], ["nl16"])
        cp(T.ar[:], T.ar32[:], ["ar32"], ["ar"])
        ts(T.we[:], T.sc3[:, 15::16], col(5), A.mult, ["sc3", "c5"], ["we"])
        if t:
            for m, (o, n) in enumerate([(-256, 256)] + SEG):
                mm(T.p2[:, 256 - n:256], T.b4[:], T.ev[:, 256 + o:256 + o + n], m == 0, m == 15, ["b4", "ev"], ["cv_"], ["p2"])
        mm(T.p3[:, 0:256], T.idfn[:], T.ax[:], False, False, ["idfn", "ax"], ["da"], ["p3"])
        mm(T.p1[:, 256:512], T.idb[:], T.xga[:], False, True, ["idb", "xga"], ["xq"], ["p1"])
        mm(T.p3[:, 0:256], T.idh[:], T.ar[:], False, True, ["idh", "ar"], ["da"], ["p3"])
        mm(T.p6[:, 0:256], T.idh[:], T.ar[:], False, True, ["idh", "ar"], ["ad"], ["p6"])
        if not last:
            act(T.nx2[:], T.nxr[:, 0:2048].indirect(T.nl16[:]), ["nxr", "nl16"], ["nx2"])
        act(T.h1[:], T.p1[:, 256:512], ["xq"], ["h1"], ["p1"], scale=0.5, bias=0.25)
        qrt = T["qr%d" % t]
        act(T.yy[:, 0::2], Q[:, 0::2], [qk, "sa%d" % t], ["yy0"], scale=0.5, bias=sa)
        act(T.h1[:], T.h1[:], ["h1"], ["h2"], bias=MAG)
        act(T.yy[:, 1::2], qrt[:], ["qr%d" % t, "ra%d" % t], ["yy1"], scale=0.5, bias=ra)
        act(T.xn[:], T.h1[:], ["h2"], ["xn"], bias=-MAG)
        act(T.y2[:], T.yy[:], ["yy0", "yy1"], ["y2"], bias=MAG)
        act(QN[:], T.y2[:], ["y2"], [qnk], bias=-MAG)
        if not last:
            act(T.qo[:], QN[:, 1::2], [qnk], ["qo"])
            send(t + 1, "q", T.qo[:], "qo", T["qr%d" % (t + 1)][:], "qr%d" % (t + 1))
            repeat_q(range(16 - GK, 16), QN, qnk)
            for k in range(16 - GK):
                act(T.q16[:, k::16], T.y2[:], ["y2"], ["q16"], bias=-MAG)
        else:
            dma("y", "out", 64, [qnk], ["yq"], T.yq[:], QN[:])
        for m, (o, n) in enumerate(SEG):
            ts(T.em[:, o:o + n], T.ar[:, 256 - n:256], T.al[:, m:m + 1], A.is_equal, ["ar", "al"], ["em%d" % m])
            mm(T.p5[:, 256 - n:256], T.b4[:], T.em[:, o:o + n], False, False, ["b4", "em%d" % m], ["ca_"], ["p5"])
        ts(T.ed[:], T.p3[:, 0:256], 0.0, A.is_equal, ["da"], ["ed"], ["p3"])
        mm(T.p5[:, 0:256], T.b4[:], T.ed[:], False, True, ["b4", "ed"], ["ca_"], ["p5"])
        tt(T.tk[:], T.p6[:, 0:256], T.oh[:], A.mult, ["ad", "oh"], ["ut"], ["p6"])
        jobs = [("ca_", "p5", T.dgt, "dgt", T.al, "al", T.ap16, "ap16", (T.dm, T.ds, T.lx))]
        if t:
            jobs = [("cv_", "p2", T.dgu, "dgu", T.vl, "vl", T.vp16, "vp16", (T.w1, T.sc1, T.d1))] + jobs
        places(jobs)
        if not last:
            cp(T.nxr[:].indirect(T.ap16[:]), T.nx2[:], ["nx2", "ap16"], ["nxr"])
            dma("y", "nd%d" % t, 16, ["nxr"], ["npf"], T.npf[:], T.nxr[0:128:16, 0:2048])
        cp(T.xt[:].indirect(T.ap16[:]), T.xn[:], ["xn", "ap16"], ["xt"])
        if last:
            dma("y", "out", 64, ["xt"], ["yx"], T.yx[:], T.xt[:, 0:2048])
        tt(T.vl[:], T.we[:], wrt[:], A.add, ["we", wk], ["vl"])
        if last:
            cp(T.vl16[:], T.vl[:], ["vl"], ["vl16"])
        tt(T.uw[:].indirect(T.vp16[:]), T.tk[:], T.dd[:], A.add, ["ut", "dd", "vp16"], ["uw"])
        if last:
            dma("y", "out", 64, ["uw"], ["yu"], T.yu[:], T.uw[:, 0:512])
        else:
            cp(T.vl16[:], T.vl[:], ["vl"], ["vl16"])
        Q, QN, qk, qnk = QN, Q, qnk, qk
    act(T.vr[:], T.idw[:].indirect(T.vl16[:]), ["idw", "vl16"], ["vr"])
    dma("y", "out", 64, ["vr"], ["yv"], T.yv[:], T.vr[0:128:16, :])
    for s in SEMAPHORES:
        if total.get(s, 0) > known["p"].get(s, 0):
            g.wait_ge(T.sem[s], total[s])
